import numpy as np
import ml_dtypes


def mxq(x, axis, fmt="e4m3"):
    dtype, down = {"e4m3": (ml_dtypes.float8_e4m3fn, 7), "e5m2": (ml_dtypes.float8_e5m2, 14)}[fmt]
    v = np.moveaxis(np.asarray(x, np.float32).astype(ml_dtypes.bfloat16).astype(np.float64), axis, -1)
    blocks = v.reshape(v.shape[:-1] + (-1, 32))
    amax = np.abs(blocks).max(-1, keepdims=True)
    byte = np.maximum(np.where(amax > 0, np.frexp(amax)[1] - 1 + 127, 0) - down, 1)
    scale = np.exp2(byte - 127.0)
    codes = (blocks / scale).astype(np.float32).astype(dtype).astype(np.float64)
    return np.moveaxis((codes * scale).reshape(v.shape), -1, axis)


WIDE = False


def mx_kscale(k):
    if not WIDE:
        return np.ones(k)
    levels = np.array([10, -10, 5, -5, 0])
    if k % 512:
        return np.exp2(np.random.permutation(np.resize(levels, k // 32))).repeat(32)
    a = np.empty((k // 512, 16))
    for p in range(k // 512):
        a[p, :8] = np.random.permutation(np.resize(levels, 8))
        for g in range(8):
            far = levels[np.abs(levels - a[p, g]) >= 10]
            a[p, g + 8] = far[np.random.randint(len(far))]
    return np.exp2(a.ravel()).repeat(32)


def f64(x):
    return np.asarray(x).astype(np.float64)


def striped(idx):
    return np.tile(idx.reshape(-1, 16).T, (8, 1)).astype(np.uint16)


def unstriped(offs):
    return offs[:16].T.reshape(-1).astype(np.int64)


def sigmoid(v):
    return 1.0 / (1.0 + np.exp(-np.maximum(v, -700.0)))


K, T, E, H, N = 512, 512, 4, 512, 512
COUNTS = (128, 384, 256, 256)
STARTS = np.cumsum((0,) + COUNTS)


def by_expert(wq, xq):
    return np.concatenate([wq[e].T @ xq[:, STARTS[e]:STARTS[e + 1]] for e in range(E)], axis=1)


def setup_inputs():
    n = np.random.standard_normal
    s = mx_kscale(K)[:, None]
    u = mx_kscale(H)
    both = np.repeat(np.arange(E), COUNTS)
    pair = np.stack([both[:T], both[T:]])[:, np.random.permutation(T)]
    pair = np.where(np.random.rand(T) < 0.5, pair, pair[::-1])
    order = np.argsort(pair.reshape(-1), kind="stable")
    slot_token = order % T; pos = np.empty(2 * T, np.int64); pos[order] = np.arange(2 * T); pos = pos.reshape(2, T)
    g = np.random.uniform(0.2, 0.8, T)
    return {
        "xT": (n((K, T)) * s).astype(np.float32),
        "w1": (n((E, K, H)) / np.sqrt(K) / s[None]).astype(np.float32),
        "w3": (n((E, K, H)) / np.sqrt(K) / s[None] * u[None, None, :]).astype(np.float32),
        "w2": (n((E, H, N)) / np.sqrt(H) / u[None, :, None]).astype(np.float32),
        "gate": np.stack([np.tile(g, (N, 1)), np.tile(1.0 - g, (N, 1))]).astype(np.float32),
        "offs": striped(slot_token),
        "pos1": striped(pos[0]),
        "pos2": striped(pos[1]),
    }


def reference(xT, w1, w3, w2, gate, offs, pos1, pos2):
    idx = unstriped(offs)
    xq = mxq(f64(xT)[:, idx], 0, "e4m3")
    h = sigmoid(by_expert(mxq(f64(w1), 1, "e4m3"), xq))
    h = h * by_expert(mxq(f64(w3), 1, "e4m3"), xq)
    y = by_expert(mxq(f64(w2), 1, "e4m3"), mxq(h, 0, "e4m3"))
    return f64(gate[0]) * y[:, unstriped(pos1)] + f64(gate[1]) * y[:, unstriped(pos2)]

@@ -1,0 +1,242 @@
+from contextlib import ExitStack
+
+import concourse.mybir as mybir
+
+K, T, E, H, N = 512, 512, 4, 512, 512
+STARTS = (0, 128, 512, 768, 1024)
+S = 1024
+
+F32 = mybir.dt.float32
+BF16 = mybir.dt.bfloat16
+U32 = mybir.dt.uint32
+U16 = mybir.dt.uint16
+U8 = mybir.dt.uint8
+I32 = mybir.dt.int32
+FP8X4 = mybir.dt.float8_e4m3fn_x4
+SIGMOID = mybir.ActivationFunctionType.Sigmoid
+MULT = mybir.AluOpType.mult
+ADD = mybir.AluOpType.add
+
+P = 128
+FLOPS = 2 * S * (2 * K * H + H * N)
+
+
+GATHERS = ((0, 512), (512, 1024))
+WINDOW = 1024
+MERGED = (0, 0, 1, 0)
+STEPS = [["gath"],["w1",2],["w3",2],["w1",1],["w3",1],["comp",2],["w1",3],["w3",3],["comp",1],["w1",0],["w3",0],["comp",3],["comp",0],["w2",0,2],["w2",0,1],["w2",0,3],["w2",0,0],["w2",1,2],["w2",1,1],["w2",1,3],["w2",1,0],["y",0],["y",1],["y",2],["y",3]]
+ORDER = (2, 1, 3, 0)
+S_X = (0, 4)
+S_W1 = (2, 2, 8, 0)
+S_W3 = (4, 8, 8, 8)
+S_W2 = ((8, 0, 8, 8), (4, 8, 8, 0))
+Q2 = (((2, 1), (3, 0)), ((0,), (1,), (2,), (3,)))
+HQ = ((0, 4), (4, 8))
+Y_COPY = (("S", "S"), ("S", "S"), ("S", "S"), ("S", "S"))
+
+
+def tile_moe_rag_glu_sigmoid_kernel(tc, xT, w1, w3, w2, gate, offs, pos1, pos2, out):
+    nc = tc.nc
+    with ExitStack() as ctx:
+        lists = ctx.enter_context(tc.tile_pool(name="lists", bufs=1))
+        keep = ctx.enter_context(tc.tile_pool(name="keep", bufs=1))
+        grouped = ctx.enter_context(tc.tile_pool(name="grouped", bufs=3))
+        grouped2 = ctx.enter_context(tc.tile_pool(name="grouped2", bufs=4))
+        double = ctx.enter_context(tc.tile_pool(name="double", bufs=2))
+        work = ctx.enter_context(tc.tile_pool(name="work", bufs=3))
+        psum = ctx.enter_context(tc.psum_pool(name="psum", bufs=8))
+
+        offs_sb = lists.tile([P, S // 16], U16, name="offs_sb")
+        pos1_sb = lists.tile([P, T // 16], U16, name="pos1_sb")
+        pos2_sb = lists.tile([P, T // 16], U16, name="pos2_sb")
+
+        warm = keep.tile([P, 1], F32, name="warm")
+        nc.gpsimd.memset(warm[:], 0.0)
+        warm_out = keep.tile([P, 1], F32, name="warm_out")
+        nc.scalar.activation(out=warm_out[:], in_=warm[:], func=SIGMOID)
+
+        def load_rows(src, cols, name):
+            t = keep.tile([P, 4, cols], F32, name=name, tag=name)
+            nc.sync.dma_start(out=t[:], in_=src.rearrange("(p j) c -> p j c", j=4))
+            return t
+
+        w1_raw, w3_raw, w2_raw, gates = {}, {}, {}, {}
+
+        def load_w2(hf):
+            for i, pair in enumerate((ORDER[:2], ORDER[2:])):
+                place = f"w{2 * i + 1}_raw{ORDER[0]}" if hf == 1 else f"w2_pair{i}"
+                raw = keep.tile([P, 2, 4, 256], F32, name=f"w2_raw{hf}_{i}", tag=place)
+                for k, e in enumerate(pair):
+                    nc.sync.dma_start(out=raw[:, k], in_=w2[e, :, hf * 256:(hf + 1) * 256].rearrange("(p j) c -> p j c", j=4))
+                    w2_raw[hf, e] = raw[:, k]
+
+        def load_gate(t):
+            if t % 2 == 0:
+                gates[t // 2] = keep.tile([P, 4, T], F32, name=f"gate{t // 2}", tag=f"w{t + 1}_raw{ORDER[1]}")
+            for c in range(2):
+                gt = gates[t // 2][:, 2 * (t % 2) + c, :]
+                nc.sync.dma_start(out=gt, in_=gate[c, t * 128:(t + 1) * 128, :])
+                gates[c, t] = gt
+
+        x_raw = []
+        for i in range(2):
+            x_raw.append(load_rows(xT[:, i * 256:(i + 1) * 256], 256, f"x_raw{i}"))
+        nc.sync.dma_start(offs_sb[:], offs)
+        for e in ORDER:
+            w1_raw[e] = load_rows(w1[e], H, f"w1_raw{e}")
+            w3_raw[e] = load_rows(w3[e], H, f"w3_raw{e}")
+        nc.sync.dma_start(pos1_sb[:], pos1)
+        nc.sync.dma_start(pos2_sb[:], pos2)
+        load_w2(0)
+        load_w2(1)
+        for t in range(0, 4):
+            load_gate(t)
+
+        def split_copy(dst, src, total, s_share):
+            if s_share:
+                nc.scalar.copy(out=dst[:, 0:s_share], in_=src[:, 0:s_share])
+            if s_share < total:
+                nc.vector.tensor_copy(out=dst[:, s_share:total], in_=src[:, s_share:total])
+
+        x_words = keep.tile([P, WINDOW], I32, name="x_words", align_bytes=64)
+        nc.vector.memset(x_words[:, T:WINDOW], 0)
+        x_codes = x_words[:].bitcast(U32)
+        x_scales = keep.tile([P, WINDOW], U8, name="x_scales", align_bytes=64)
+        nc.gpsimd.memset(x_scales[:], 0)
+        g_codes = keep.tile([P, S], U32, name="g_codes", align_bytes=64)
+        g_scales = keep.tile([P, S], U8, name="g_scales", align_bytes=64)
+        h_bf = keep.tile([P, S, 4], BF16, name="h_bf", align_bytes=64)
+        h_codes = keep.tile([P, S], U32, name="h_codes", align_bytes=64)
+        h_scales = keep.tile([P, S], U8, name="h_scales", align_bytes=64)
+
+        xg = keep.tile([P, T, 4], BF16, name="xg", align_bytes=64)
+        for i in range(2):
+            half = slice(i * 256, (i + 1) * 256)
+            split_copy(xg[:, half, :].rearrange("p (c i) j -> p c j i", i=4), x_raw[i][:].rearrange("p j (c i) -> p c j i", i=4), 64, 8 * S_X[i])
+            nc.vector.quantize_mx(out=x_words[:, half].bitcast(FP8X4), scales=x_scales[:, half], in_=xg[:, half, :].rearrange("p c j -> p (c j)"))
+
+        def gather(a, b):
+            idx = offs_sb[:, a // 16:b // 16]
+            nc.vector.tensor_copy(out=g_codes[:, a:b], in_=x_codes.indirect(idx))
+            nc.vector.tensor_copy(out=g_scales[:, a:b], in_=x_scales[:].indirect(idx))
+
+        pair_open = {}
+
+        def one_weight(raws, nm, e, s_share):
+            if MERGED[e]:
+                if e not in pair_open:
+                    wd = double.tile([P, 2, 4, 128, 4], BF16, name="wd", align_bytes=64)
+                    codes = keep.tile([P, 2, 512], U32, name=f"w13_{e}_codes", align_bytes=64)
+                    scales = keep.tile([P, 2, 512], U8, name=f"w13_{e}_scales", align_bytes=64)
+                    pair_open[e] = [wd, codes, scales, 0]
+                wd, codes, scales, n = pair_open[e]
+                i = 0 if nm == "w1" else 1
+                split_copy(wd[:, i].rearrange("p t m j -> p m j t"),
+                           raws[e][:].rearrange("p j (m t) -> p m j t", t=4), 128, 16 * s_share)
+                pair_open[e][3] = n + 1
+                if n == 1:
+                    nc.vector.quantize_mx(out=codes[:].rearrange("p w c -> p (w c)").bitcast(FP8X4),
+                                          scales=scales[:].rearrange("p w c -> p (w c)"),
+                                          in_=wd[:].rearrange("p w t m j -> p (w t m j)"))
+                return codes[:, i, :], scales[:, i, :]
+            wg = grouped.tile([P, 4, 128, 4], BF16, name="wg", align_bytes=64)
+            split_copy(wg[:].rearrange("p t m j -> p m j t"),
+                       raws[e][:].rearrange("p j (m t) -> p m j t", t=4), 128, 16 * s_share)
+            codes = keep.tile([P, 512], U32, name=f"{nm}_{e}_codes", align_bytes=64)
+            scales = keep.tile([P, 512], U8, name=f"{nm}_{e}_scales", align_bytes=64)
+            nc.vector.quantize_mx(out=codes[:].bitcast(FP8X4), scales=scales[:],
+                                  in_=wg[:].rearrange("p t m j -> p (t m j)"))
+            return codes[:], scales[:]
+
+        w2q = {}
+
+        w2_open = {}
+
+        def w2_step(hf, e):
+            for group in Q2[hf]:
+                if e not in group:
+                    continue
+                k = len(group)
+                if (hf, group) not in w2_open:
+                    wg = grouped2.tile([P, k, 256, 4], BF16, name="w2g", align_bytes=64)
+                    w2_open[hf, group] = [wg, 0]
+                wg = w2_open[hf, group][0]
+                split_copy(wg[:, group.index(e)].rearrange("p (c i) j -> p c j i", i=4),
+                           w2_raw[hf, e].rearrange("p j (c i) -> p c j i", i=4), 64, 8 * S_W2[hf][e])
+                w2_open[hf, group][1] += 1
+                if w2_open[hf, group][1] == k:
+                    codes = keep.tile([P, k * 256], U32, name=f"w2_codes{hf}_{group[0]}", align_bytes=64)
+                    scales = keep.tile([P, k * 256], U8, name=f"w2_scales{hf}_{group[0]}", align_bytes=64)
+                    nc.vector.quantize_mx(out=codes[:].bitcast(FP8X4), scales=scales[:],
+                                          in_=wg[:].rearrange("p k c j -> p (k c j)"))
+                    for i, g in enumerate(group):
+                        w2q[hf, g] = (codes, scales, i * 256)
+
+        done = set()
+
+        def hidden(e, w1c, w1s, w3c, w3s):
+            for chunk in range(STARTS[e] // 128, STARTS[e + 1] // 128):
+                slots = slice(chunk * 128, (chunk + 1) * 128)
+                pa = psum.tile([P, 4, 128], F32, name="pa", tag="bank")
+                pb = psum.tile([P, 4, 128], F32, name="pb", tag="bank")
+                for acc, codes, scales in ((pa, w1c, w1s), (pb, w3c, w3s)):
+                    for t in range(4):
+                        cols = slice(t * 128, (t + 1) * 128)
+                        nc.tensor.matmul_mx(out=acc[:, t, :],
+                                            lhsT=codes[:, cols].bitcast(FP8X4), lhsT_scale=scales[:, cols],
+                                            rhs=g_codes[:, slots].bitcast(FP8X4), rhs_scale=g_scales[:, slots],
+                                            start=True, stop=True)
+                sig = work.tile([P, 128, 4], F32, name="sig")
+                nc.scalar.activation(out=sig[:], in_=pa[:].rearrange("p t n -> p n t"), func=SIGMOID)
+                nc.vector.tensor_tensor(out=h_bf[:, slots, :], in0=pb[:].rearrange("p t n -> p n t"), in1=sig[:], op=MULT)
+                done.add(chunk)
+                for a, b in HQ:
+                    if a <= chunk < b and all(i in done for i in range(a, b)):
+                        hs = slice(a * 128, b * 128)
+                        nc.vector.quantize_mx(out=h_codes[:, hs].bitcast(FP8X4), scales=h_scales[:, hs],
+                                              in_=h_bf[:, hs, :].rearrange("p n t -> p (n t)"))
+
+
+        def outputs(t):
+            y = keep.tile([P, S], F32, name=f"y{t}")
+            for bank in range(2):
+                py = psum.tile([P, 512], F32, name=f"py{bank}", tag="bank")
+                for e, c0, c1 in (((0, 0, 128), (1, 128, 256), (1, 256, 512)), ((2, 512, 768), (3, 768, 1024)))[bank]:
+                    codes, scales, base = w2q[t // 2, e]
+                    cols = slice(base + (t % 2) * 128, base + (t % 2) * 128 + 128)
+                    nc.tensor.matmul_mx(out=py[:, c0 - bank * 512:c1 - bank * 512],
+                                        lhsT=codes[:, cols].bitcast(FP8X4), lhsT_scale=scales[:, cols],
+                                        rhs=h_codes[:, c0:c1].bitcast(FP8X4), rhs_scale=h_scales[:, c0:c1],
+                                        start=True, stop=True)
+                if Y_COPY[t][bank] == "S":
+                    nc.scalar.copy(out=y[:, bank * 512:(bank + 1) * 512], in_=py[:])
+                else:
+                    nc.vector.tensor_copy(out=y[:, bank * 512:(bank + 1) * 512], in_=py[:])
+            r1 = work.tile([P, T], F32, name="r1")
+            r2 = work.tile([P, T], F32, name="r2")
+            nc.vector.tensor_tensor(out=r1[:], in0=y[:].indirect(pos1_sb[:]), in1=gates[0, t], op=MULT)
+            nc.vector.tensor_tensor(out=r2[:], in0=y[:].indirect(pos2_sb[:]), in1=gates[1, t], op=MULT)
+            pieces = 2 if t == 3 else 1
+            for i in range(pieces):
+                cols = slice(i * T // pieces, (i + 1) * T // pieces)
+                nc.vector.tensor_tensor(out=r1[:, cols], in0=r1[:, cols], in1=r2[:, cols], op=ADD)
+                nc.sync.dma_start(out=out[t * 128:(t + 1) * 128, cols], in_=r1[:, cols])
+
+        weights = {}
+        for step in STEPS:
+            kind, args = step[0], step[1:]
+            if kind == "gath":
+                for a, b in GATHERS:
+                    gather(a, b)
+            elif kind == "g1":
+                gather(*GATHERS[args[0]])
+            elif kind == "w1":
+                weights["w1", args[0]] = one_weight(w1_raw, "w1", args[0], S_W1[args[0]])
+            elif kind == "w3":
+                weights["w3", args[0]] = one_weight(w3_raw, "w3", args[0], S_W3[args[0]])
+            elif kind == "comp":
+                hidden(args[0], *weights["w1", args[0]], *weights["w3", args[0]])
+            elif kind == "w2":
+                w2_step(args[0], args[1])
+            else:
+                outputs(args[0])

@@ -11,7 +11,6 @@ BF16 = mybir.dt.bfloat16
 U32 = mybir.dt.uint32
 U16 = mybir.dt.uint16
 U8 = mybir.dt.uint8
-I32 = mybir.dt.int32
 FP8X4 = mybir.dt.float8_e4m3fn_x4
 SIGMOID = mybir.ActivationFunctionType.Sigmoid
 MULT = mybir.AluOpType.mult
@@ -20,19 +19,15 @@ ADD = mybir.AluOpType.add
 P = 128
 FLOPS = 2 * S * (2 * K * H + H * N)
 
-
-GATHERS = ((0, 512), (512, 1024))
-WINDOW = 1024
-MERGED = (0, 0, 1, 0)
-STEPS = [["gath"],["w1",2],["w3",2],["w1",1],["w3",1],["comp",2],["w1",3],["w3",3],["comp",1],["w1",0],["w3",0],["comp",3],["comp",0],["w2",0,2],["w2",0,1],["w2",0,3],["w2",0,0],["w2",1,2],["w2",1,1],["w2",1,3],["w2",1,0],["y",0],["y",1],["y",2],["y",3]]
-ORDER = (2, 1, 3, 0)
-S_X = (0, 4)
-S_W1 = (2, 2, 8, 0)
-S_W3 = (4, 8, 8, 8)
-S_W2 = ((8, 0, 8, 8), (4, 8, 8, 0))
-Q2 = (((2, 1), (3, 0)), ((0,), (1,), (2,), (3,)))
-HQ = ((0, 4), (4, 8))
-Y_COPY = (("S", "S"), ("S", "S"), ("S", "S"), ("S", "S"))
+ORDER = (1, 2, 3, 0)
+SH = (128, 128, 0, 128, 32, 128, 32, 64)
+CUT = 320
+NQ = 0
+EARLY = True
+Q10 = True
+LAST_SHARE = 40
+ON_SCALAR_BUFS = 10
+ON_VECTOR_BUFS = 36
 
 
 def tile_moe_rag_glu_sigmoid_kernel(tc, xT, w1, w3, w2, gate, offs, pos1, pos2, out):
@@ -40,11 +35,15 @@ def tile_moe_rag_glu_sigmoid_kernel(tc, xT, w1, w3, w2, gate, offs, pos1, pos2, 
     with ExitStack() as ctx:
         lists = ctx.enter_context(tc.tile_pool(name="lists", bufs=1))
         keep = ctx.enter_context(tc.tile_pool(name="keep", bufs=1))
-        grouped = ctx.enter_context(tc.tile_pool(name="grouped", bufs=3))
-        grouped2 = ctx.enter_context(tc.tile_pool(name="grouped2", bufs=4))
-        double = ctx.enter_context(tc.tile_pool(name="double", bufs=2))
-        work = ctx.enter_context(tc.tile_pool(name="work", bufs=3))
+        by_scalar = ctx.enter_context(tc.tile_pool(name="by_scalar", bufs=ON_SCALAR_BUFS))
+        by_vector = ctx.enter_context(tc.tile_pool(name="by_vector", bufs=ON_VECTOR_BUFS))
         psum = ctx.enter_context(tc.psum_pool(name="psum", bufs=8))
+
+        def s_tile(shape, dtype, name):
+            return by_scalar.tile(shape, dtype, name=name, tag="s", align_bytes=64)
+
+        def v_tile(shape, dtype, name):
+            return by_vector.tile(shape, dtype, name=name, tag="v", align_bytes=64)
 
         offs_sb = lists.tile([P, S // 16], U16, name="offs_sb")
         pos1_sb = lists.tile([P, T // 16], U16, name="pos1_sb")
@@ -54,189 +53,204 @@ def tile_moe_rag_glu_sigmoid_kernel(tc, xT, w1, w3, w2, gate, offs, pos1, pos2, 
         nc.gpsimd.memset(warm[:], 0.0)
         warm_out = keep.tile([P, 1], F32, name="warm_out")
         nc.scalar.activation(out=warm_out[:], in_=warm[:], func=SIGMOID)
+        x_scales = keep.tile([P, T], U8, name="x_scales", align_bytes=64)
+        nc.gpsimd.memset(x_scales[:], 0)
 
-        def load_rows(src, cols, name):
-            t = keep.tile([P, 4, cols], F32, name=name, tag=name)
-            nc.sync.dma_start(out=t[:], in_=src.rearrange("(p j) c -> p j c", j=4))
-            return t
+        def load_rows(dst, src):
+            nc.sync.dma_start(out=dst, in_=src.rearrange("(p j) c -> p j c", j=4))
 
-        w1_raw, w3_raw, w2_raw, gates = {}, {}, {}, {}
-
-        def load_w2(hf):
-            for i, pair in enumerate((ORDER[:2], ORDER[2:])):
-                place = f"w{2 * i + 1}_raw{ORDER[0]}" if hf == 1 else f"w2_pair{i}"
-                raw = keep.tile([P, 2, 4, 256], F32, name=f"w2_raw{hf}_{i}", tag=place)
-                for k, e in enumerate(pair):
-                    nc.sync.dma_start(out=raw[:, k], in_=w2[e, :, hf * 256:(hf + 1) * 256].rearrange("(p j) c -> p j c", j=4))
-                    w2_raw[hf, e] = raw[:, k]
-
-        def load_gate(t):
-            if t % 2 == 0:
-                gates[t // 2] = keep.tile([P, 4, T], F32, name=f"gate{t // 2}", tag=f"w{t + 1}_raw{ORDER[1]}")
-            for c in range(2):
-                gt = gates[t // 2][:, 2 * (t % 2) + c, :]
-                nc.sync.dma_start(out=gt, in_=gate[c, t * 128:(t + 1) * 128, :])
-                gates[c, t] = gt
-
-        x_raw = []
+        x_raw, w_raw, w2_raw = [], {}, {}
         for i in range(2):
-            x_raw.append(load_rows(xT[:, i * 256:(i + 1) * 256], 256, f"x_raw{i}"))
+            x_raw.append(keep.tile([P, 4, 256], F32, name=f"x_raw{i}"))
+            load_rows(x_raw[i][:], xT[:, i * 256:(i + 1) * 256])
         nc.sync.dma_start(offs_sb[:], offs)
         for e in ORDER:
-            w1_raw[e] = load_rows(w1[e], H, f"w1_raw{e}")
-            w3_raw[e] = load_rows(w3[e], H, f"w3_raw{e}")
-        nc.sync.dma_start(pos1_sb[:], pos1)
-        nc.sync.dma_start(pos2_sb[:], pos2)
-        load_w2(0)
-        load_w2(1)
-        for t in range(0, 4):
-            load_gate(t)
+            for nm, w in (("w1", w1), ("w3", w3)):
+                w_raw[nm, e] = keep.tile([P, 4, H], F32, name=f"{nm}_raw{e}")
+                load_rows(w_raw[nm, e][:], w[e])
+        gate_sb = keep.tile([P, 2, T], F32, name="gate_sb")
+        for t in range(4):
+            for pair in (1, 0):
+                w2_raw[t, pair] = keep.tile([P, 2, 4, P], F32, name=f"w2_raw{t}{pair}")
+                for k in (1, 0):
+                    load_rows(w2_raw[t, pair][:, k], w2[2 * pair + k, :, t * P:(t + 1) * P])
+            if t == 0:
+                nc.sync.dma_start(pos1_sb[:], pos1)
+                nc.sync.dma_start(pos2_sb[:], pos2)
+                nc.sync.dma_start(out=gate_sb[:], in_=gate[:, 0:P, :].rearrange("c p t -> p c t"))
 
-        def split_copy(dst, src, total, s_share):
-            if s_share:
-                nc.scalar.copy(out=dst[:, 0:s_share], in_=src[:, 0:s_share])
-            if s_share < total:
-                nc.vector.tensor_copy(out=dst[:, s_share:total], in_=src[:, s_share:total])
-
-        x_words = keep.tile([P, WINDOW], I32, name="x_words", align_bytes=64)
-        nc.vector.memset(x_words[:, T:WINDOW], 0)
-        x_codes = x_words[:].bitcast(U32)
-        x_scales = keep.tile([P, WINDOW], U8, name="x_scales", align_bytes=64)
-        nc.gpsimd.memset(x_scales[:], 0)
-        g_codes = keep.tile([P, S], U32, name="g_codes", align_bytes=64)
-        g_scales = keep.tile([P, S], U8, name="g_scales", align_bytes=64)
-        h_bf = keep.tile([P, S, 4], BF16, name="h_bf", align_bytes=64)
-        h_codes = keep.tile([P, S], U32, name="h_codes", align_bytes=64)
-        h_scales = keep.tile([P, S], U8, name="h_scales", align_bytes=64)
-
-        xg = keep.tile([P, T, 4], BF16, name="xg", align_bytes=64)
+        x_words = None
         for i in range(2):
             half = slice(i * 256, (i + 1) * 256)
-            split_copy(xg[:, half, :].rearrange("p (c i) j -> p c j i", i=4), x_raw[i][:].rearrange("p j (c i) -> p c j i", i=4), 64, 8 * S_X[i])
-            nc.vector.quantize_mx(out=x_words[:, half].bitcast(FP8X4), scales=x_scales[:, half], in_=xg[:, half, :].rearrange("p c j -> p (c j)"))
+            xg = v_tile([P, 256, 4], BF16, f"xg{i}")
+            nc.vector.tensor_copy(out=xg[:].rearrange("p (c i) j -> p c j i", i=4), in_=x_raw[i][:].rearrange("p j (c i) -> p c j i", i=4))
+            if i == 0:
+                x_words = v_tile([P, T], U32, "x_words")
+            nc.vector.quantize_mx(out=x_words[:, half].bitcast(FP8X4), scales=x_scales[:, half], in_=xg[:].rearrange("p c j -> p (c j)"))
 
-        def gather(a, b):
+        g_codes, g_scales = {}, {}
+
+        def gather(e):
+            a, b = STARTS[e], STARTS[e + 1]
             idx = offs_sb[:, a // 16:b // 16]
-            nc.vector.tensor_copy(out=g_codes[:, a:b], in_=x_codes.indirect(idx))
-            nc.vector.tensor_copy(out=g_scales[:, a:b], in_=x_scales[:].indirect(idx))
+            g_codes[e] = v_tile([P, b - a], U32, f"g_codes{e}")
+            nc.vector.tensor_copy(out=g_codes[e][:], in_=x_words[:].indirect(idx))
+            g_scales[e] = v_tile([P, b - a], U8, f"g_scales{e}")
+            nc.vector.tensor_copy(out=g_scales[e][:], in_=x_scales[:].indirect(idx))
 
-        pair_open = {}
+        grouped, wq = {}, {}
 
-        def one_weight(raws, nm, e, s_share):
-            if MERGED[e]:
-                if e not in pair_open:
-                    wd = double.tile([P, 2, 4, 128, 4], BF16, name="wd", align_bytes=64)
-                    codes = keep.tile([P, 2, 512], U32, name=f"w13_{e}_codes", align_bytes=64)
-                    scales = keep.tile([P, 2, 512], U8, name=f"w13_{e}_scales", align_bytes=64)
-                    pair_open[e] = [wd, codes, scales, 0]
-                wd, codes, scales, n = pair_open[e]
-                i = 0 if nm == "w1" else 1
-                split_copy(wd[:, i].rearrange("p t m j -> p m j t"),
-                           raws[e][:].rearrange("p j (m t) -> p m j t", t=4), 128, 16 * s_share)
-                pair_open[e][3] = n + 1
-                if n == 1:
-                    nc.vector.quantize_mx(out=codes[:].rearrange("p w c -> p (w c)").bitcast(FP8X4),
-                                          scales=scales[:].rearrange("p w c -> p (w c)"),
-                                          in_=wd[:].rearrange("p w t m j -> p (w t m j)"))
-                return codes[:, i, :], scales[:, i, :]
-            wg = grouped.tile([P, 4, 128, 4], BF16, name="wg", align_bytes=64)
-            split_copy(wg[:].rearrange("p t m j -> p m j t"),
-                       raws[e][:].rearrange("p j (m t) -> p m j t", t=4), 128, 16 * s_share)
-            codes = keep.tile([P, 512], U32, name=f"{nm}_{e}_codes", align_bytes=64)
-            scales = keep.tile([P, 512], U8, name=f"{nm}_{e}_scales", align_bytes=64)
+        def group(nm, e, share):
+            wg = s_tile([P, 4, 128, 4], BF16, f"g{nm}{e}")
+            dst = wg[:].rearrange("p t m j -> p m j t")
+            src = w_raw[nm, e][:].rearrange("p j (m t) -> p m j t", t=4)
+            if share > 0:
+                nc.scalar.copy(out=dst[:, 0:share], in_=src[:, 0:share])
+            if share < 128:
+                nc.vector.tensor_copy(out=dst[:, share:128], in_=src[:, share:128])
+            grouped[nm, e] = wg
+
+        def quantise(nm, e):
+            codes = v_tile([P, 512], U32, f"q{nm}{e}")
+            scales = keep.tile([P, 512], U8, name=f"{nm}_scales{e}", align_bytes=64)
             nc.vector.quantize_mx(out=codes[:].bitcast(FP8X4), scales=scales[:],
-                                  in_=wg[:].rearrange("p t m j -> p (t m j)"))
-            return codes[:], scales[:]
+                                  in_=grouped[nm, e][:].rearrange("p t m j -> p (t m j)"))
+            wq[nm, e] = (codes, scales)
 
-        w2q = {}
+        def chunks(e):
+            return range(STARTS[e] // P, STARTS[e + 1] // P)
 
-        w2_open = {}
+        banks, sigs, h_bf, h_codes = {}, {}, {}, {}
+        h_scales = {}
 
-        def w2_step(hf, e):
-            for group in Q2[hf]:
-                if e not in group:
-                    continue
-                k = len(group)
-                if (hf, group) not in w2_open:
-                    wg = grouped2.tile([P, k, 256, 4], BF16, name="w2g", align_bytes=64)
-                    w2_open[hf, group] = [wg, 0]
-                wg = w2_open[hf, group][0]
-                split_copy(wg[:, group.index(e)].rearrange("p (c i) j -> p c j i", i=4),
-                           w2_raw[hf, e].rearrange("p j (c i) -> p c j i", i=4), 64, 8 * S_W2[hf][e])
-                w2_open[hf, group][1] += 1
-                if w2_open[hf, group][1] == k:
-                    codes = keep.tile([P, k * 256], U32, name=f"w2_codes{hf}_{group[0]}", align_bytes=64)
-                    scales = keep.tile([P, k * 256], U8, name=f"w2_scales{hf}_{group[0]}", align_bytes=64)
-                    nc.vector.quantize_mx(out=codes[:].bitcast(FP8X4), scales=scales[:],
-                                          in_=wg[:].rearrange("p k c j -> p (k c j)"))
-                    for i, g in enumerate(group):
-                        w2q[hf, g] = (codes, scales, i * 256)
+        def products(nm, e):
+            codes, scales = wq[nm, e]
+            for chunk in chunks(e):
+                slots = slice(chunk * P - STARTS[e], (chunk + 1) * P - STARTS[e])
+                acc = psum.tile([P, 4, P], F32, name=f"p{nm}{chunk}", tag="bank")
+                for t in range(4):
+                    cols = slice(t * P, (t + 1) * P)
+                    nc.tensor.matmul_mx(out=acc[:, t, :],
+                                        lhsT=codes[:, cols].bitcast(FP8X4), lhsT_scale=scales[:, cols],
+                                        rhs=g_codes[e][:, slots].bitcast(FP8X4), rhs_scale=g_scales[e][:, slots],
+                                        start=True, stop=True)
+                banks[nm, chunk] = acc
 
-        done = set()
+        def sigmoids(e):
+            for chunk in chunks(e):
+                sigs[chunk] = s_tile([P, P, 4], F32, f"sig{chunk}")
+                nc.scalar.activation(out=sigs[chunk][:], in_=banks["w1", chunk][:].rearrange("p t n -> p n t"), func=SIGMOID)
 
-        def hidden(e, w1c, w1s, w3c, w3s):
-            for chunk in range(STARTS[e] // 128, STARTS[e + 1] // 128):
-                slots = slice(chunk * 128, (chunk + 1) * 128)
-                pa = psum.tile([P, 4, 128], F32, name="pa", tag="bank")
-                pb = psum.tile([P, 4, 128], F32, name="pb", tag="bank")
-                for acc, codes, scales in ((pa, w1c, w1s), (pb, w3c, w3s)):
-                    for t in range(4):
-                        cols = slice(t * 128, (t + 1) * 128)
-                        nc.tensor.matmul_mx(out=acc[:, t, :],
-                                            lhsT=codes[:, cols].bitcast(FP8X4), lhsT_scale=scales[:, cols],
-                                            rhs=g_codes[:, slots].bitcast(FP8X4), rhs_scale=g_scales[:, slots],
-                                            start=True, stop=True)
-                sig = work.tile([P, 128, 4], F32, name="sig")
-                nc.scalar.activation(out=sig[:], in_=pa[:].rearrange("p t n -> p n t"), func=SIGMOID)
-                nc.vector.tensor_tensor(out=h_bf[:, slots, :], in0=pb[:].rearrange("p t n -> p n t"), in1=sig[:], op=MULT)
-                done.add(chunk)
-                for a, b in HQ:
-                    if a <= chunk < b and all(i in done for i in range(a, b)):
-                        hs = slice(a * 128, b * 128)
-                        nc.vector.quantize_mx(out=h_codes[:, hs].bitcast(FP8X4), scales=h_scales[:, hs],
-                                              in_=h_bf[:, hs, :].rearrange("p n t -> p (n t)"))
+        def gated(chunk):
+            h_bf[chunk] = v_tile([P, P, 4], BF16, f"h_bf{chunk}")
+            nc.vector.tensor_tensor(out=h_bf[chunk][:], in0=banks["w3", chunk][:].rearrange("p t n -> p n t"), in1=sigs[chunk][:], op=MULT)
 
+        def quantise_h(chunk):
+            h_codes[chunk] = v_tile([P, P], U32, f"hq{chunk}")
+            h_scales[chunk] = keep.tile([P, P], U8, name=f"h_scales{chunk}", align_bytes=64)
+            nc.vector.quantize_mx(out=h_codes[chunk][:].bitcast(FP8X4), scales=h_scales[chunk][:],
+                                  in_=h_bf[chunk][:].rearrange("p n t -> p (n t)"))
+
+        w2g, w2q = {}, {}
+
+        def group_w2(t, pair, on_scalar):
+            wg = (s_tile if on_scalar else v_tile)([P, 2, P, 4], BF16, f"gw2{t}{pair}")
+            dst = wg[:].rearrange("p k (c i) j -> p k c j i", i=4)
+            src = w2_raw[t, pair][:].rearrange("p k j (c i) -> p k c j i", i=4)
+            if on_scalar:
+                nc.scalar.copy(out=dst, in_=src)
+            else:
+                nc.vector.tensor_copy(out=dst, in_=src)
+            w2g[t, pair] = wg
+
+        def quantise_w2(t, pair):
+            codes = v_tile([P, 2 * P], U32, f"qw2{t}{pair}")
+            scales = keep.tile([P, 2 * P], U8, name=f"w2_scales{t}{pair}", align_bytes=64)
+            nc.vector.quantize_mx(out=codes[:].bitcast(FP8X4), scales=scales[:],
+                                  in_=w2g[t, pair][:].rearrange("p k c j -> p (k c j)"))
+            w2q[t, pair] = (codes, scales)
+
+        ys, parts = {}, {}
 
         def outputs(t):
-            y = keep.tile([P, S], F32, name=f"y{t}")
-            for bank in range(2):
-                py = psum.tile([P, 512], F32, name=f"py{bank}", tag="bank")
-                for e, c0, c1 in (((0, 0, 128), (1, 128, 256), (1, 256, 512)), ((2, 512, 768), (3, 768, 1024)))[bank]:
-                    codes, scales, base = w2q[t // 2, e]
-                    cols = slice(base + (t % 2) * 128, base + (t % 2) * 128 + 128)
-                    nc.tensor.matmul_mx(out=py[:, c0 - bank * 512:c1 - bank * 512],
-                                        lhsT=codes[:, cols].bitcast(FP8X4), lhsT_scale=scales[:, cols],
-                                        rhs=h_codes[:, c0:c1].bitcast(FP8X4), rhs_scale=h_scales[:, c0:c1],
-                                        start=True, stop=True)
-                if Y_COPY[t][bank] == "S":
-                    nc.scalar.copy(out=y[:, bank * 512:(bank + 1) * 512], in_=py[:])
-                else:
-                    nc.vector.tensor_copy(out=y[:, bank * 512:(bank + 1) * 512], in_=py[:])
-            r1 = work.tile([P, T], F32, name="r1")
-            r2 = work.tile([P, T], F32, name="r2")
-            nc.vector.tensor_tensor(out=r1[:], in0=y[:].indirect(pos1_sb[:]), in1=gates[0, t], op=MULT)
-            nc.vector.tensor_tensor(out=r2[:], in0=y[:].indirect(pos2_sb[:]), in1=gates[1, t], op=MULT)
-            pieces = 2 if t == 3 else 1
-            for i in range(pieces):
-                cols = slice(i * T // pieces, (i + 1) * T // pieces)
-                nc.vector.tensor_tensor(out=r1[:, cols], in0=r1[:, cols], in1=r2[:, cols], op=ADD)
-                nc.sync.dma_start(out=out[t * 128:(t + 1) * 128, cols], in_=r1[:, cols])
+            ys[t] = s_tile([P, S], F32, f"y{t}")
+            for bank in (1, 0):
+                py = psum.tile([P, 512], F32, name=f"py{t}{bank}", tag="bank")
+                codes, scales = w2q[t, bank]
+                for k in (1, 0):
+                    cols = slice(k * P, (k + 1) * P)
+                    for chunk in chunks(2 * bank + k):
+                        place = chunk * P - bank * 512
+                        nc.tensor.matmul_mx(out=py[:, place:place + P],
+                                            lhsT=codes[:, cols].bitcast(FP8X4), lhsT_scale=scales[:, cols],
+                                            rhs=h_codes[chunk][:].bitcast(FP8X4), rhs_scale=h_scales[chunk][:],
+                                            start=True, stop=True)
+                nc.scalar.copy(out=ys[t][:, bank * 512:(bank + 1) * 512], in_=py[:])
 
-        weights = {}
-        for step in STEPS:
-            kind, args = step[0], step[1:]
-            if kind == "gath":
-                for a, b in GATHERS:
-                    gather(a, b)
-            elif kind == "g1":
-                gather(*GATHERS[args[0]])
-            elif kind == "w1":
-                weights["w1", args[0]] = one_weight(w1_raw, "w1", args[0], S_W1[args[0]])
-            elif kind == "w3":
-                weights["w3", args[0]] = one_weight(w3_raw, "w3", args[0], S_W3[args[0]])
-            elif kind == "comp":
-                hidden(args[0], *weights["w1", args[0]], *weights["w3", args[0]])
-            elif kind == "w2":
-                w2_step(args[0], args[1])
-            else:
-                outputs(args[0])
+        def fetch(t, c, a=0, b=T):
+            parts[t, c, a] = v_tile([P, b - a], F32, f"r{t}{c}{a}")
+            idx = (pos1_sb, pos2_sb)[c][:, a // 16:b // 16]
+            nc.vector.tensor_tensor(out=parts[t, c, a][:], in0=ys[t][:].indirect(idx), in1=gate_sb[:, c, a:b], op=MULT)
+
+        def finish(t, a=0, b=T):
+            total = v_tile([P, b - a], F32, f"sum{t}{a}")
+            nc.vector.tensor_tensor(out=total[:], in0=parts[t, 0, a][:], in1=parts[t, 1, a][:], op=ADD)
+            nc.sync.dma_start(out=out[t * P:(t + 1) * P, a:b], in_=total[:])
+
+        first, last = ORDER[0], ORDER[-1]
+        gather(ORDER[0])
+        gather(ORDER[1])
+        previous = None
+        for i, e in enumerate(ORDER):
+            group("w1", e, SH[2 * i])
+            if previous is not None:
+                quantise("w3", previous)
+                products("w3", previous)
+            quantise("w1", e)
+            products("w1", e)
+            if i < 2:
+                gather(ORDER[i + 2])
+            group("w3", e, SH[2 * i + 1])
+            if e == last and EARLY:
+                group_w2(0, 1, True)
+            sigmoids(e)
+            if previous is not None:
+                for n, chunk in enumerate(chunks(previous)):
+                    gated(chunk)
+                    if e == last and n == NQ:
+                        quantise("w3", e)
+                        products("w3", e)
+                for chunk in chunks(previous):
+                    quantise_h(chunk)
+            previous = e
+        if not EARLY:
+            group_w2(0, 1, True)
+        group_w2(0, 0, True)
+        gated(chunks(last)[0])
+        quantise_w2(0, 1)
+        quantise_h(chunks(last)[0])
+        quantise_w2(0, 0)
+        outputs(0)
+        group_w2(1, 1, False)
+        group_w2(1, 0, False)
+        quantise_w2(1, 1)
+        for t in range(3):
+            fetch(t, 0)
+            quantise_w2(t + 1, 0)
+            if t < 2:
+                group_w2(t + 2, 1, True)
+            outputs(t + 1)
+            if t < 2:
+                group_w2(t + 2, 0, True)
+            if t > 0:
+                finish(t - 1)
+            fetch(t, 1)
+            if t < 2:
+                quantise_w2(t + 2, 1)
+        fetch(3, 0, 0, CUT)
+        finish(2)
+        fetch(3, 1, 0, CUT)
+        fetch(3, 0, CUT, T)
+        finish(3, 0, CUT)
+        fetch(3, 1, CUT, T)
+        finish(3, CUT, T)

@@ -1,6 +1,7 @@
 from contextlib import ExitStack
 
 import concourse.mybir as mybir
+from concourse.masks import make_identity
 
 K, T, E, H, N = 512, 512, 4, 512, 512
 STARTS = (0, 128, 512, 768, 1024)
@@ -20,8 +21,11 @@ P = 128
 FLOPS = 2 * S * (2 * K * H + H * N)
 
 ORDER = (1, 2, 3, 0)
-SH = (128, 128, 0, 128, 32, 128, 32, 64)
+SH = (128, 128, 0, 128, 48, 128, 48, 72)
 CUT = 320
+W2_ORDER = (2, 3, 1, 0)
+X_SHARE = 44
+A = True
 NQ = 0
 EARLY = True
 Q10 = True
@@ -49,6 +53,9 @@ def tile_moe_rag_glu_sigmoid_kernel(tc, xT, w1, w3, w2, gate, offs, pos1, pos2, 
         pos1_sb = lists.tile([P, T // 16], U16, name="pos1_sb")
         pos2_sb = lists.tile([P, T // 16], U16, name="pos2_sb")
 
+        gate_rows = keep.tile([P, 2, P], F32, name="gate_rows")
+        nc.gpsimd.memset(gate_rows[:], 0.0)
+        nc.scalar.dma_start(out=gate_rows[0:4], in_=gate[:, 0, :].rearrange("c (b i) -> b c i", b=4))
         warm = keep.tile([P, 1], F32, name="warm")
         nc.gpsimd.memset(warm[:], 0.0)
         warm_out = keep.tile([P, 1], F32, name="warm_out")
@@ -59,34 +66,49 @@ def tile_moe_rag_glu_sigmoid_kernel(tc, xT, w1, w3, w2, gate, offs, pos1, pos2, 
         def load_rows(dst, src):
             nc.sync.dma_start(out=dst, in_=src.rearrange("(p j) c -> p j c", j=4))
 
-        x_raw, w_raw, w2_raw = [], {}, {}
-        for i in range(2):
-            x_raw.append(keep.tile([P, 4, 256], F32, name=f"x_raw{i}"))
-            load_rows(x_raw[i][:], xT[:, i * 256:(i + 1) * 256])
+        identity = keep.tile([P, P], F32, name="identity")
+        make_identity(nc, identity[:])
+
+        w_raw, w2_raw = {}, {}
+        x_raw = keep.tile([P, 4, T], F32, name="x_raw")
+        load_rows(x_raw[:], xT)
         nc.sync.dma_start(offs_sb[:], offs)
         for e in ORDER:
             for nm, w in (("w1", w1), ("w3", w3)):
                 w_raw[nm, e] = keep.tile([P, 4, H], F32, name=f"{nm}_raw{e}")
                 load_rows(w_raw[nm, e][:], w[e])
-        gate_sb = keep.tile([P, 2, T], F32, name="gate_sb")
-        for t in range(4):
-            for pair in (1, 0):
-                w2_raw[t, pair] = keep.tile([P, 2, 4, P], F32, name=f"w2_raw{t}{pair}")
-                for k in (1, 0):
-                    load_rows(w2_raw[t, pair][:, k], w2[2 * pair + k, :, t * P:(t + 1) * P])
-            if t == 0:
+            if e == ORDER[1]:
                 nc.sync.dma_start(pos1_sb[:], pos1)
                 nc.sync.dma_start(pos2_sb[:], pos2)
-                nc.sync.dma_start(out=gate_sb[:], in_=gate[:, 0:P, :].rearrange("c p t -> p c t"))
+        for half in range(2):
+            for e in W2_ORDER:
+                w2_raw[half, e] = keep.tile([P, 4, 256], F32, name=f"w2_raw{half}{e}")
+                load_rows(w2_raw[half, e][:], w2[e, :, half * 256:(half + 1) * 256])
 
-        x_words = None
-        for i in range(2):
-            half = slice(i * 256, (i + 1) * 256)
-            xg = v_tile([P, 256, 4], BF16, f"xg{i}")
-            nc.vector.tensor_copy(out=xg[:].rearrange("p (c i) j -> p c j i", i=4), in_=x_raw[i][:].rearrange("p j (c i) -> p c j i", i=4))
-            if i == 0:
-                x_words = v_tile([P, T], U32, "x_words")
-            nc.vector.quantize_mx(out=x_words[:, half].bitcast(FP8X4), scales=x_scales[:, half], in_=xg[:].rearrange("p c j -> p (c j)"))
+        turned = psum.tile([P, 2, P], F32, name="turned", tag="bank")
+        for c in range(2):
+            nc.tensor.transpose(turned[:, c, :], gate_rows[:, c, :], identity[:])
+        gate_cols = s_tile([P, 2, 4], F32, "gate_cols")
+        nc.scalar.copy(out=gate_cols[:], in_=turned[:, :, 0:4])
+        gate_sb = {}
+
+        def spread_gate(c):
+            spread = psum.tile([P, 4, P], F32, name=f"spread{c}", tag="bank")
+            for b in range(4):
+                nc.tensor.transpose(spread[:, b, :], gate_cols[:, c, b:b + 1].to_broadcast([P, P]), identity[:])
+            gate_sb[c] = keep.tile([P, T], F32, name=f"gate_sb{c}")
+            nc.scalar.copy(out=gate_sb[c][:], in_=spread[:].rearrange("p b i -> p (b i)"))
+
+        spread_gate(0)
+
+        xg = s_tile([P, T, 4], BF16, "xg")
+        dst = xg[:].rearrange("p (c i) j -> p c j i", i=4)
+        src = x_raw[:].rearrange("p j (c i) -> p c j i", i=4)
+        nc.scalar.copy(out=dst[:, 0:X_SHARE], in_=src[:, 0:X_SHARE])
+        nc.vector.tensor_copy(out=dst[:, X_SHARE:128], in_=src[:, X_SHARE:128])
+        spread_gate(1)
+        x_words = v_tile([P, T], U32, "x_words")
+        nc.vector.quantize_mx(out=x_words[:].bitcast(FP8X4), scales=x_scales[:], in_=xg[:].rearrange("p c j -> p (c j)"))
 
         g_codes, g_scales = {}, {}
 
@@ -153,44 +175,45 @@ def tile_moe_rag_glu_sigmoid_kernel(tc, xT, w1, w3, w2, gate, offs, pos1, pos2, 
 
         w2g, w2q = {}, {}
 
-        def group_w2(t, pair, on_scalar):
-            wg = (s_tile if on_scalar else v_tile)([P, 2, P, 4], BF16, f"gw2{t}{pair}")
-            dst = wg[:].rearrange("p k (c i) j -> p k c j i", i=4)
-            src = w2_raw[t, pair][:].rearrange("p k j (c i) -> p k c j i", i=4)
+        def group_w2(half, e, on_scalar):
+            wg = (s_tile if on_scalar else v_tile)([P, 256, 4], BF16, f"gw2{half}{e}")
+            dst = wg[:].rearrange("p (c i) j -> p c j i", i=4)
+            src = w2_raw[half, e][:].rearrange("p j (c i) -> p c j i", i=4)
             if on_scalar:
                 nc.scalar.copy(out=dst, in_=src)
             else:
                 nc.vector.tensor_copy(out=dst, in_=src)
-            w2g[t, pair] = wg
+            w2g[half, e] = wg
 
-        def quantise_w2(t, pair):
-            codes = v_tile([P, 2 * P], U32, f"qw2{t}{pair}")
-            scales = keep.tile([P, 2 * P], U8, name=f"w2_scales{t}{pair}", align_bytes=64)
+        def quantise_w2(half, e):
+            codes = v_tile([P, 256], U32, f"qw2{half}{e}")
+            scales = keep.tile([P, 256], U8, name=f"w2_scales{half}{e}", align_bytes=64)
             nc.vector.quantize_mx(out=codes[:].bitcast(FP8X4), scales=scales[:],
-                                  in_=w2g[t, pair][:].rearrange("p k c j -> p (k c j)"))
-            w2q[t, pair] = (codes, scales)
+                                  in_=w2g[half, e][:].rearrange("p c j -> p (c j)"))
+            w2q[half, e] = (codes, scales)
 
         ys, parts = {}, {}
 
-        def outputs(t):
-            ys[t] = s_tile([P, S], F32, f"y{t}")
-            for bank in (1, 0):
-                py = psum.tile([P, 512], F32, name=f"py{t}{bank}", tag="bank")
-                codes, scales = w2q[t, bank]
-                for k in (1, 0):
-                    cols = slice(k * P, (k + 1) * P)
-                    for chunk in chunks(2 * bank + k):
-                        place = chunk * P - bank * 512
-                        nc.tensor.matmul_mx(out=py[:, place:place + P],
-                                            lhsT=codes[:, cols].bitcast(FP8X4), lhsT_scale=scales[:, cols],
-                                            rhs=h_codes[chunk][:].bitcast(FP8X4), rhs_scale=h_scales[chunk][:],
-                                            start=True, stop=True)
-                nc.scalar.copy(out=ys[t][:, bank * 512:(bank + 1) * 512], in_=py[:])
+        def outputs(t, experts):
+            if t not in ys:
+                ys[t] = s_tile([P, S], F32, f"y{t}")
+            a, b = STARTS[experts[0]], STARTS[experts[-1] + 1]
+            py = psum.tile([P, b - a], F32, name=f"py{t}{experts[0]}", tag="bank")
+            cols = slice((t % 2) * P, (t % 2 + 1) * P)
+            for e in experts:
+                codes, scales = w2q[t // 2, e]
+                for chunk in chunks(e):
+                    place = chunk * P - a
+                    nc.tensor.matmul_mx(out=py[:, place:place + P],
+                                        lhsT=codes[:, cols].bitcast(FP8X4), lhsT_scale=scales[:, cols],
+                                        rhs=h_codes[chunk][:].bitcast(FP8X4), rhs_scale=h_scales[chunk][:],
+                                        start=True, stop=True)
+            nc.scalar.copy(out=ys[t][:, a:b], in_=py[:])
 
         def fetch(t, c, a=0, b=T):
             parts[t, c, a] = v_tile([P, b - a], F32, f"r{t}{c}{a}")
             idx = (pos1_sb, pos2_sb)[c][:, a // 16:b // 16]
-            nc.vector.tensor_tensor(out=parts[t, c, a][:], in0=ys[t][:].indirect(idx), in1=gate_sb[:, c, a:b], op=MULT)
+            nc.vector.tensor_tensor(out=parts[t, c, a][:], in0=ys[t][:].indirect(idx), in1=gate_sb[c][:, a:b], op=MULT)
 
         def finish(t, a=0, b=T):
             total = v_tile([P, b - a], F32, f"sum{t}{a}")
@@ -211,8 +234,8 @@ def tile_moe_rag_glu_sigmoid_kernel(tc, xT, w1, w3, w2, gate, offs, pos1, pos2, 
             if i < 2:
                 gather(ORDER[i + 2])
             group("w3", e, SH[2 * i + 1])
-            if e == last and EARLY:
-                group_w2(0, 1, True)
+            if e == last:
+                group_w2(0, 2, True)
             sigmoids(e)
             if previous is not None:
                 for n, chunk in enumerate(chunks(previous)):
@@ -223,30 +246,40 @@ def tile_moe_rag_glu_sigmoid_kernel(tc, xT, w1, w3, w2, gate, offs, pos1, pos2, 
                 for chunk in chunks(previous):
                     quantise_h(chunk)
             previous = e
-        if not EARLY:
-            group_w2(0, 1, True)
-        group_w2(0, 0, True)
+        quantise_w2(0, 2)
         gated(chunks(last)[0])
-        quantise_w2(0, 1)
+        group_w2(0, 3, True)
         quantise_h(chunks(last)[0])
+        quantise_w2(0, 3)
+        group_w2(0, 1, True)
+        outputs(0, (2, 3))
+        outputs(1, (2, 3))
+        quantise_w2(0, 1)
+        group_w2(0, 0, False)
+        outputs(0, (1,))
         quantise_w2(0, 0)
-        outputs(0)
-        group_w2(1, 1, False)
-        group_w2(1, 0, False)
+        outputs(0, (0,))
+        outputs(1, (0, 1))
+        group_w2(1, 2, True)
+        fetch(0, 0)
+        group_w2(1, 3, True)
+        fetch(0, 1)
+        quantise_w2(1, 2)
+        fetch(1, 0)
+        group_w2(1, 1, True)
+        group_w2(1, 0, True)
+        quantise_w2(1, 3)
+        outputs(2, (2, 3))
+        finish(0)
         quantise_w2(1, 1)
-        for t in range(3):
-            fetch(t, 0)
-            quantise_w2(t + 1, 0)
-            if t < 2:
-                group_w2(t + 2, 1, True)
-            outputs(t + 1)
-            if t < 2:
-                group_w2(t + 2, 0, True)
-            if t > 0:
-                finish(t - 1)
-            fetch(t, 1)
-            if t < 2:
-                quantise_w2(t + 2, 1)
+        quantise_w2(1, 0)
+        outputs(2, (0, 1))
+        outputs(3, (2, 3))
+        outputs(3, (0, 1))
+        fetch(1, 1)
+        finish(1)
+        fetch(2, 0)
+        fetch(2, 1)
         fetch(3, 0, 0, CUT)
         finish(2)
         fetch(3, 1, 0, CUT)

@@ -53,9 +53,6 @@ def tile_moe_rag_glu_sigmoid_kernel(tc, xT, w1, w3, w2, gate, offs, pos1, pos2, 
         pos1_sb = lists.tile([P, T // 16], U16, name="pos1_sb")
         pos2_sb = lists.tile([P, T // 16], U16, name="pos2_sb")
 
-        gate_rows = keep.tile([P, 2, P], F32, name="gate_rows")
-        nc.gpsimd.memset(gate_rows[:], 0.0)
-        nc.scalar.dma_start(out=gate_rows[0:4], in_=gate[:, 0, :].rearrange("c (b i) -> b c i", b=4))
         warm = keep.tile([P, 1], F32, name="warm")
         nc.gpsimd.memset(warm[:], 0.0)
         warm_out = keep.tile([P, 1], F32, name="warm_out")
@@ -72,6 +69,8 @@ def tile_moe_rag_glu_sigmoid_kernel(tc, xT, w1, w3, w2, gate, offs, pos1, pos2, 
         w_raw, w2_raw = {}, {}
         x_raw = keep.tile([P, 4, T], F32, name="x_raw")
         load_rows(x_raw[:], xT)
+        gate_cols = keep.tile([P, 2, 8], F32, name="gate_cols")
+        nc.sync.dma_start(out=gate_cols[:, :, 0:4], in_=gate[:, 0, :].rearrange("c (p j) -> p c j", j=4))
         nc.sync.dma_start(offs_sb[:], offs)
         for e in ORDER:
             for nm, w in (("w1", w1), ("w3", w3)):
@@ -85,27 +84,22 @@ def tile_moe_rag_glu_sigmoid_kernel(tc, xT, w1, w3, w2, gate, offs, pos1, pos2, 
                 w2_raw[half, e] = keep.tile([P, 4, 256], F32, name=f"w2_raw{half}{e}")
                 load_rows(w2_raw[half, e][:], w2[e, :, half * 256:(half + 1) * 256])
 
-        turned = psum.tile([P, 2, P], F32, name="turned", tag="bank")
-        for c in range(2):
-            nc.tensor.transpose(turned[:, c, :], gate_rows[:, c, :], identity[:])
-        gate_cols = s_tile([P, 2, 4], F32, "gate_cols")
-        nc.scalar.copy(out=gate_cols[:], in_=turned[:, :, 0:4])
         gate_sb = {}
 
         def spread_gate(c):
             spread = psum.tile([P, 4, P], F32, name=f"spread{c}", tag="bank")
             for b in range(4):
                 nc.tensor.transpose(spread[:, b, :], gate_cols[:, c, b:b + 1].to_broadcast([P, P]), identity[:])
-            gate_sb[c] = keep.tile([P, T], F32, name=f"gate_sb{c}")
-            nc.scalar.copy(out=gate_sb[c][:], in_=spread[:].rearrange("p b i -> p (b i)"))
+            gate_sb[c] = s_tile([P, T], F32, f"gate_sb{c}")
+            nc.scalar.copy(out=gate_sb[c][:].rearrange("p (i b) -> p i b", b=4), in_=spread[:].rearrange("p b i -> p i b"))
 
-        spread_gate(0)
 
         xg = s_tile([P, T, 4], BF16, "xg")
         dst = xg[:].rearrange("p (c i) j -> p c j i", i=4)
         src = x_raw[:].rearrange("p j (c i) -> p c j i", i=4)
         nc.scalar.copy(out=dst[:, 0:X_SHARE], in_=src[:, 0:X_SHARE])
         nc.vector.tensor_copy(out=dst[:, X_SHARE:128], in_=src[:, X_SHARE:128])
+        spread_gate(0)
         spread_gate(1)
         x_words = v_tile([P, T], U32, "x_words")
         nc.vector.quantize_mx(out=x_words[:].bitcast(FP8X4), scales=x_scales[:], in_=xg[:].rearrange("p c j -> p (c j)"))

@@ -169,40 +169,46 @@ def tile_moe_rag_glu_sigmoid_kernel(tc, xT, w1, w3, w2, gate, offs, pos1, pos2, 
 
         w2g, w2q = {}, {}
 
-        def group_w2(half, e, on_scalar):
-            wg = (s_tile if on_scalar else v_tile)([P, 256, 4], BF16, f"gw2{half}{e}")
+        def group_w2(half, e, engine, a=0, b=256, pool=None):
+            if pool is None:
+                wg = (s_tile if engine is nc.scalar else v_tile)([P, b - a, 4], BF16, f"gw2{half}{e}{a}")
+            else:
+                wg = pool.tile([P, b - a, 4], BF16, name=f"gw2{half}{e}{a}", tag="late", align_bytes=64)
             dst = wg[:].rearrange("p (c i) j -> p c j i", i=4)
-            src = w2_raw[half, e][:].rearrange("p j (c i) -> p c j i", i=4)
-            if on_scalar:
+            src = w2_raw[half, e][:, :, a:b].rearrange("p j (c i) -> p c j i", i=4)
+            if engine is nc.scalar:
                 nc.scalar.copy(out=dst, in_=src)
             else:
                 nc.vector.tensor_copy(out=dst, in_=src)
-            w2g[half, e] = wg
+            w2g[half, e, a] = wg
 
-        def quantise_w2(half, e):
-            codes = v_tile([P, 256], U32, f"qw2{half}{e}")
-            scales = keep.tile([P, 256], U8, name=f"w2_scales{half}{e}", align_bytes=64)
+        def quantise_w2(half, e, a=0, b=256):
+            codes = v_tile([P, b - a], U32, f"qw2{half}{e}{a}")
+            scales = keep.tile([P, b - a], U8, name=f"w2_scales{half}{e}{a}", align_bytes=64)
             nc.vector.quantize_mx(out=codes[:].bitcast(FP8X4), scales=scales[:],
-                                  in_=w2g[half, e][:].rearrange("p c j -> p (c j)"))
-            w2q[half, e] = (codes, scales)
+                                  in_=w2g[half, e, a][:].rearrange("p c j -> p (c j)"))
+            for col in range(a, b, P):
+                w2q[2 * half + col // P, e] = (codes[:, col - a:col - a + P], scales[:, col - a:col - a + P])
 
         ys, parts = {}, {}
 
-        def outputs(t, experts):
+        def outputs(t, experts, engine=nc.scalar):
             if t not in ys:
                 ys[t] = s_tile([P, S], F32, f"y{t}")
             a, b = STARTS[experts[0]], STARTS[experts[-1] + 1]
             py = psum.tile([P, b - a], F32, name=f"py{t}{experts[0]}", tag="bank")
-            cols = slice((t % 2) * P, (t % 2 + 1) * P)
             for e in experts:
-                codes, scales = w2q[t // 2, e]
+                codes, scales = w2q[t, e]
                 for chunk in chunks(e):
                     place = chunk * P - a
                     nc.tensor.matmul_mx(out=py[:, place:place + P],
-                                        lhsT=codes[:, cols].bitcast(FP8X4), lhsT_scale=scales[:, cols],
+                                        lhsT=codes.bitcast(FP8X4), lhsT_scale=scales,
                                         rhs=h_codes[chunk][:].bitcast(FP8X4), rhs_scale=h_scales[chunk][:],
                                         start=True, stop=True)
-            nc.scalar.copy(out=ys[t][:, a:b], in_=py[:])
+            if engine is nc.scalar:
+                nc.scalar.copy(out=ys[t][:, a:b], in_=py[:])
+            else:
+                nc.vector.tensor_copy(out=ys[t][:, a:b], in_=py[:])
 
         def fetch(t, c, a=0, b=T):
             parts[t, c, a] = v_tile([P, b - a], F32, f"r{t}{c}{a}")
@@ -229,7 +235,7 @@ def tile_moe_rag_glu_sigmoid_kernel(tc, xT, w1, w3, w2, gate, offs, pos1, pos2, 
                 gather(ORDER[i + 2])
             group("w3", e, SH[2 * i + 1])
             if e == last:
-                group_w2(0, 2, True)
+                group_w2(0, 2, nc.scalar)
             sigmoids(e)
             if previous is not None:
                 for n, chunk in enumerate(chunks(previous)):
@@ -242,35 +248,40 @@ def tile_moe_rag_glu_sigmoid_kernel(tc, xT, w1, w3, w2, gate, offs, pos1, pos2, 
             previous = e
         quantise_w2(0, 2)
         gated(chunks(last)[0])
-        group_w2(0, 3, True)
+        group_w2(0, 3, nc.scalar)
         quantise_h(chunks(last)[0])
         quantise_w2(0, 3)
-        group_w2(0, 1, True)
+        group_w2(0, 1, nc.scalar)
         outputs(0, (2, 3))
         outputs(1, (2, 3))
         quantise_w2(0, 1)
-        group_w2(0, 0, False)
         outputs(0, (1,))
-        quantise_w2(0, 0)
-        outputs(0, (0,))
+        group_w2(0, 0, nc.vector, 0, P)
+        group_w2(0, 0, nc.vector, P, 256, keep)
+        quantise_w2(0, 0, 0, P)
+        quantise_w2(0, 0, P, 256)
+        outputs(0, (0,), nc.vector)
+        group_w2(1, 2, nc.scalar, 0, 256, keep)
         outputs(1, (0, 1))
-        group_w2(1, 2, True)
         fetch(0, 0)
-        group_w2(1, 3, True)
-        fetch(0, 1)
+        group_w2(1, 3, nc.scalar)
         quantise_w2(1, 2)
-        fetch(1, 0)
-        group_w2(1, 1, True)
-        group_w2(1, 0, True)
+        fetch(0, 1)
+        group_w2(1, 1, nc.scalar)
         quantise_w2(1, 3)
         outputs(2, (2, 3))
-        finish(0)
+        fetch(1, 0)
+        group_w2(1, 0, nc.scalar, 0, P)
         quantise_w2(1, 1)
-        quantise_w2(1, 0)
-        outputs(2, (0, 1))
+        outputs(2, (1,))
+        finish(0)
+        group_w2(1, 0, nc.scalar, P, 256)
+        quantise_w2(1, 0, 0, P)
+        outputs(2, (0,))
         outputs(3, (2, 3))
-        outputs(3, (0, 1))
         fetch(1, 1)
+        quantise_w2(1, 0, P, 256)
+        outputs(3, (0, 1))
         finish(1)
         fetch(2, 0)
         fetch(2, 1)

@@ -21,17 +21,19 @@ P = 128
 FLOPS = 2 * S * (2 * K * H + H * N)
 
 ORDER = (1, 2, 3, 0)
-SH = (128, 128, 0, 128, 48, 128, 48, 72)
+SH = (128, 128, 0, 128, 48, 128, 48, 96)
 CUT = 320
 W2_ORDER = (2, 3, 1, 0)
 X_SHARE = 44
 A = True
+S1 = 0
+S3 = 64
 NQ = 0
 EARLY = True
 Q10 = True
 LAST_SHARE = 40
-ON_SCALAR_BUFS = 10
-ON_VECTOR_BUFS = 36
+ON_SCALAR_BUFS = 11
+ON_VECTOR_BUFS = 34
 
 
 def tile_moe_rag_glu_sigmoid_kernel(tc, xT, w1, w3, w2, gate, offs, pos1, pos2, out):
@@ -72,17 +74,28 @@ def tile_moe_rag_glu_sigmoid_kernel(tc, xT, w1, w3, w2, gate, offs, pos1, pos2, 
         gate_cols = keep.tile([P, 2, 8], F32, name="gate_cols")
         nc.sync.dma_start(out=gate_cols[:, :, 0:4], in_=gate[:, 0, :].rearrange("c (p j) -> p c j", j=4))
         nc.sync.dma_start(offs_sb[:], offs)
-        for e in ORDER:
+        first, second, third, last = ORDER
+
+        def load_w2(e, a, b):
+            raw = keep.tile([P, 4, b - a], F32, name=f"w2_raw{e}_{a}")
+            load_rows(raw[:], w2[e, :, a:b])
+            for col in range(a, b, P):
+                w2_raw[e, col] = (raw, a)
+
+        for i, e in enumerate(ORDER):
             for nm, w in (("w1", w1), ("w3", w3)):
                 w_raw[nm, e] = keep.tile([P, 4, H], F32, name=f"{nm}_raw{e}")
                 load_rows(w_raw[nm, e][:], w[e])
-            if e == ORDER[1]:
+            if e == second:
                 nc.sync.dma_start(pos1_sb[:], pos1)
                 nc.sync.dma_start(pos2_sb[:], pos2)
-        for half in range(2):
-            for e in W2_ORDER:
-                w2_raw[half, e] = keep.tile([P, 4, 256], F32, name=f"w2_raw{half}{e}")
-                load_rows(w2_raw[half, e][:], w2[e, :, half * 256:(half + 1) * 256])
+        load_w2(first, 0, N)
+        load_w2(second, 0, N)
+        load_w2(third, 0, 256)
+        load_w2(last, 0, 128)
+        load_w2(last, 128, 256)
+        load_w2(third, 256, 512)
+        load_w2(last, 256, 512)
 
         gate_sb = {}
 
@@ -169,26 +182,27 @@ def tile_moe_rag_glu_sigmoid_kernel(tc, xT, w1, w3, w2, gate, offs, pos1, pos2, 
 
         w2g, w2q = {}, {}
 
-        def group_w2(half, e, engine, a=0, b=256, pool=None):
-            if pool is None:
-                wg = (s_tile if engine is nc.scalar else v_tile)([P, b - a, 4], BF16, f"gw2{half}{e}{a}")
+        def group_w2(e, a, b, engine, shared=False):
+            if shared:
+                wg = keep.tile([P, b - a, 4], BF16, name=f"gw2{e}_{a}", tag="shared", align_bytes=64)
             else:
-                wg = pool.tile([P, b - a, 4], BF16, name=f"gw2{half}{e}{a}", tag="late", align_bytes=64)
+                wg = (s_tile if engine is nc.scalar else v_tile)([P, b - a, 4], BF16, f"gw2{e}_{a}")
+            raw, start = w2_raw[e, a]
             dst = wg[:].rearrange("p (c i) j -> p c j i", i=4)
-            src = w2_raw[half, e][:, :, a:b].rearrange("p j (c i) -> p c j i", i=4)
+            src = raw[:, :, a - start:b - start].rearrange("p j (c i) -> p c j i", i=4)
             if engine is nc.scalar:
                 nc.scalar.copy(out=dst, in_=src)
             else:
                 nc.vector.tensor_copy(out=dst, in_=src)
-            w2g[half, e, a] = wg
+            w2g[e, a] = wg
 
-        def quantise_w2(half, e, a=0, b=256):
-            codes = v_tile([P, b - a], U32, f"qw2{half}{e}{a}")
-            scales = keep.tile([P, b - a], U8, name=f"w2_scales{half}{e}{a}", align_bytes=64)
+        def quantise_w2(e, a, b):
+            codes = v_tile([P, b - a], U32, f"qw2{e}_{a}")
+            scales = keep.tile([P, b - a], U8, name=f"w2_scales{e}_{a}", align_bytes=64)
             nc.vector.quantize_mx(out=codes[:].bitcast(FP8X4), scales=scales[:],
-                                  in_=w2g[half, e, a][:].rearrange("p c j -> p (c j)"))
+                                  in_=w2g[e, a][:].rearrange("p c j -> p (c j)"))
             for col in range(a, b, P):
-                w2q[2 * half + col // P, e] = (codes[:, col - a:col - a + P], scales[:, col - a:col - a + P])
+                w2q[col // P, e] = (codes[:, col - a:col - a + P], scales[:, col - a:col - a + P])
 
         ys, parts = {}, {}
 
@@ -220,69 +234,99 @@ def tile_moe_rag_glu_sigmoid_kernel(tc, xT, w1, w3, w2, gate, offs, pos1, pos2, 
             nc.vector.tensor_tensor(out=total[:], in0=parts[t, 0, a][:], in1=parts[t, 1, a][:], op=ADD)
             nc.sync.dma_start(out=out[t * P:(t + 1) * P, a:b], in_=total[:])
 
-        first, last = ORDER[0], ORDER[-1]
-        gather(ORDER[0])
-        gather(ORDER[1])
+        turned, summed = {}, {}
+
+        def turn_and_add(t):
+            turned[t] = psum.tile([P, 4, P], F32, name=f"turned{t}", tag="bank")
+            for b in range(4):
+                for c in range(2):
+                    nc.tensor.matmul(out=turned[t][:, b, :], lhsT=parts[t, c, 0][:, b * P:(b + 1) * P], rhs=identity[:],
+                                     start=(c == 0), stop=(c == 1), is_transpose=True)
+
+        def turn_back(t):
+            by_token = s_tile([P, 4, P], F32, f"by_token{t}")
+            nc.scalar.copy(out=by_token[:], in_=turned[t][:])
+            summed[t] = psum.tile([P, 4, P], F32, name=f"summed{t}", tag="bank")
+            for b in range(4):
+                nc.tensor.transpose(summed[t][:, b, :], by_token[:, b, :], identity[:])
+
+        def store(t):
+            total = s_tile([P, T], F32, f"total{t}")
+            nc.scalar.copy(out=total[:], in_=summed[t][:].rearrange("p b i -> p (b i)"))
+            nc.sync.dma_start(out=out[t * P:(t + 1) * P, :], in_=total[:])
+
+        def ready(nm, e):
+            quantise(nm, e)
+            products(nm, e)
+
+        def hidden(e):
+            for chunk in chunks(e):
+                gated(chunk)
+
+        def hidden_codes(e):
+            for chunk in chunks(e):
+                quantise_h(chunk)
+
+        gather(first)
+        gather(second)
         previous = None
         for i, e in enumerate(ORDER):
             group("w1", e, SH[2 * i])
             if previous is not None:
-                quantise("w3", previous)
-                products("w3", previous)
-            quantise("w1", e)
-            products("w1", e)
+                ready("w3", previous)
+            ready("w1", e)
             if i < 2:
                 gather(ORDER[i + 2])
             group("w3", e, SH[2 * i + 1])
-            if e == last:
-                group_w2(0, 2, nc.scalar)
             sigmoids(e)
             if previous is not None:
-                for n, chunk in enumerate(chunks(previous)):
-                    gated(chunk)
-                    if e == last and n == NQ:
-                        quantise("w3", e)
-                        products("w3", e)
-                for chunk in chunks(previous):
-                    quantise_h(chunk)
+                hidden(previous)
+                hidden_codes(previous)
             previous = e
-        quantise_w2(0, 2)
-        gated(chunks(last)[0])
-        group_w2(0, 3, nc.scalar)
-        quantise_h(chunks(last)[0])
-        quantise_w2(0, 3)
-        group_w2(0, 1, nc.scalar)
-        outputs(0, (2, 3))
-        outputs(1, (2, 3))
-        quantise_w2(0, 1)
-        outputs(0, (1,))
-        group_w2(0, 0, nc.vector, 0, P)
-        group_w2(0, 0, nc.vector, P, 256, keep)
-        quantise_w2(0, 0, 0, P)
-        quantise_w2(0, 0, P, 256)
-        outputs(0, (0,), nc.vector)
-        group_w2(1, 2, nc.scalar, 0, 256, keep)
-        outputs(1, (0, 1))
+        ready("w3", last)
+        group_w2(first, 0, 256, nc.scalar)
+        group_w2(first, 256, N, nc.scalar)
+        hidden(last)
+        quantise_w2(first, 0, 256)
+        hidden_codes(last)
+        group_w2(second, 0, 256, nc.vector)
+        group_w2(second, 256, N, nc.scalar)
+        quantise_w2(first, 256, N)
+        outputs(0, (first,))
+        quantise_w2(second, 0, 256)
+        group_w2(third, 0, 128, nc.vector)
+        quantise_w2(second, 256, N)
+        group_w2(third, 128, 256, nc.scalar)
+        quantise_w2(third, 0, 128)
+        outputs(1, (first,))
+        group_w2(last, 0, 128, nc.vector, True)
+        outputs(0, (second, third))
+        quantise_w2(third, 128, 256)
+        quantise_w2(last, 0, 128)
+        group_w2(last, 128, 256, nc.scalar, True)
+        outputs(0, (last,), nc.vector)
+        outputs(1, (second, third))
         fetch(0, 0)
-        group_w2(1, 3, nc.scalar)
-        quantise_w2(1, 2)
+        quantise_w2(last, 128, 256)
+        group_w2(third, 256, N, nc.scalar)
+        outputs(1, (last,))
+        outputs(2, (first,))
         fetch(0, 1)
-        group_w2(1, 1, nc.scalar)
-        quantise_w2(1, 3)
-        outputs(2, (2, 3))
+        quantise_w2(third, 256, N)
+        group_w2(last, 256, N, nc.scalar)
+        outputs(2, (second, third))
+        outputs(3, (second, third))
         fetch(1, 0)
-        group_w2(1, 0, nc.scalar, 0, P)
-        quantise_w2(1, 1)
-        outputs(2, (1,))
-        finish(0)
-        group_w2(1, 0, nc.scalar, P, 256)
-        quantise_w2(1, 0, 0, P)
-        outputs(2, (0,))
-        outputs(3, (2, 3))
+        quantise_w2(last, 256, N)
+        outputs(2, (last,))
+        outputs(3, (last, first))
         fetch(1, 1)
-        quantise_w2(1, 0, P, 256)
-        outputs(3, (0, 1))
-        finish(1)
+        turn_and_add(0)
+        turn_and_add(1)
+        turn_back(0)
+        turn_back(1)
+        store(0)
+        store(1)
         fetch(2, 0)
         fetch(2, 1)
         fetch(3, 0, 0, CUT)

@@ -21,13 +21,14 @@ P = 128
 FLOPS = 2 * S * (2 * K * H + H * N)
 
 ORDER = (1, 2, 3, 0)
-SH = (128, 128, 0, 128, 48, 128, 48, 96)
+SH = (128, 128, 32, 128, 40, 128, 40, 80)
 CUT = 320
 W2_ORDER = (2, 3, 1, 0)
 X_SHARE = 44
 A = True
 S1 = 0
 S3 = 64
+N1 = 1
 NQ = 0
 EARLY = True
 Q10 = True
@@ -269,34 +270,40 @@ def tile_moe_rag_glu_sigmoid_kernel(tc, xT, w1, w3, w2, gate, offs, pos1, pos2, 
 
         gather(first)
         gather(second)
-        previous = None
-        for i, e in enumerate(ORDER):
+        group("w1", first, 128)
+        ready("w1", first)
+        gather(third)
+        group("w3", first, 128)
+        sigmoids(first)
+        for i in range(1, E):
+            previous, e = ORDER[i - 1], ORDER[i]
+            ready("w3", previous)
             group("w1", e, SH[2 * i])
-            if previous is not None:
-                ready("w3", previous)
+            if e == second:
+                gather(last)
+            for chunk in chunks(previous)[:N1]:
+                gated(chunk)
             ready("w1", e)
-            if i < 2:
-                gather(ORDER[i + 2])
             group("w3", e, SH[2 * i + 1])
             sigmoids(e)
-            if previous is not None:
-                hidden(previous)
+            for chunk in chunks(previous)[N1:]:
+                gated(chunk)
+            if e != last:
                 hidden_codes(previous)
-            previous = e
         ready("w3", last)
+        hidden_codes(third)
         group_w2(first, 0, 256, nc.scalar)
         group_w2(first, 256, N, nc.scalar)
         hidden(last)
         quantise_w2(first, 0, 256)
-        hidden_codes(last)
         group_w2(second, 0, 256, nc.vector)
         group_w2(second, 256, N, nc.scalar)
-        quantise_w2(first, 256, N)
+        hidden_codes(last)
         outputs(0, (first,))
         quantise_w2(second, 0, 256)
         group_w2(third, 0, 128, nc.vector)
-        quantise_w2(second, 256, N)
         group_w2(third, 128, 256, nc.scalar)
+        quantise_w2(first, 256, N)
         quantise_w2(third, 0, 128)
         outputs(1, (first,))
         group_w2(last, 0, 128, nc.vector, True)
@@ -304,6 +311,7 @@ def tile_moe_rag_glu_sigmoid_kernel(tc, xT, w1, w3, w2, gate, offs, pos1, pos2, 
         quantise_w2(third, 128, 256)
         quantise_w2(last, 0, 128)
         group_w2(last, 128, 256, nc.scalar, True)
+        quantise_w2(second, 256, N)
         outputs(0, (last,), nc.vector)
         outputs(1, (second, third))
         fetch(0, 0)

@@ -21,13 +21,15 @@ P = 128
 FLOPS = 2 * S * (2 * K * H + H * N)
 
 ORDER = (1, 2, 3, 0)
-SH = (128, 128, 32, 128, 40, 128, 40, 80)
+SH = (128, 112, 32, 128, 32, 128, 32, 80)
 CUT = 320
 W2_ORDER = (2, 3, 1, 0)
 X_SHARE = 44
 A = True
 S1 = 0
 S3 = 64
+W2S = (0, 128, 0, 128, 0, 128, 0, 128, 128, 128)
+NADD = 2
 N1 = 1
 NQ = 0
 EARLY = True
@@ -183,18 +185,19 @@ def tile_moe_rag_glu_sigmoid_kernel(tc, xT, w1, w3, w2, gate, offs, pos1, pos2, 
 
         w2g, w2q = {}, {}
 
-        def group_w2(e, a, b, engine, shared=False):
+        def group_w2(e, a, b, share, shared=False):
             if shared:
                 wg = keep.tile([P, b - a, 4], BF16, name=f"gw2{e}_{a}", tag="shared", align_bytes=64)
             else:
-                wg = (s_tile if engine is nc.scalar else v_tile)([P, b - a, 4], BF16, f"gw2{e}_{a}")
+                wg = (s_tile if share else v_tile)([P, b - a, 4], BF16, f"gw2{e}_{a}")
             raw, start = w2_raw[e, a]
             dst = wg[:].rearrange("p (c i) j -> p c j i", i=4)
             src = raw[:, :, a - start:b - start].rearrange("p j (c i) -> p c j i", i=4)
-            if engine is nc.scalar:
-                nc.scalar.copy(out=dst, in_=src)
-            else:
-                nc.vector.tensor_copy(out=dst, in_=src)
+            h = (b - a) // 4 * share // 128
+            if h > 0:
+                nc.scalar.copy(out=dst[:, 0:h], in_=src[:, 0:h])
+            if h < (b - a) // 4:
+                nc.vector.tensor_copy(out=dst[:, h:], in_=src[:, h:])
             w2g[e, a] = wg
 
         def quantise_w2(e, a, b):
@@ -268,12 +271,13 @@ def tile_moe_rag_glu_sigmoid_kernel(tc, xT, w1, w3, w2, gate, offs, pos1, pos2, 
             for chunk in chunks(e):
                 quantise_h(chunk)
 
+        eng = {"S": nc.scalar, "V": nc.vector}
         gather(first)
         gather(second)
-        group("w1", first, 128)
+        group("w1", first, SH[0])
         ready("w1", first)
         gather(third)
-        group("w3", first, 128)
+        group("w3", first, SH[1])
         sigmoids(first)
         for i in range(1, E):
             previous, e = ORDER[i - 1], ORDER[i]
@@ -291,51 +295,55 @@ def tile_moe_rag_glu_sigmoid_kernel(tc, xT, w1, w3, w2, gate, offs, pos1, pos2, 
             if e != last:
                 hidden_codes(previous)
         ready("w3", last)
+        group_w2(first, 0, 256, W2S[0])
+        group_w2(first, 256, N, W2S[1])
+        group_w2(second, 256, N, W2S[3])
         hidden_codes(third)
-        group_w2(first, 0, 256, nc.scalar)
-        group_w2(first, 256, N, nc.scalar)
-        hidden(last)
         quantise_w2(first, 0, 256)
-        group_w2(second, 0, 256, nc.vector)
-        group_w2(second, 256, N, nc.scalar)
-        hidden_codes(last)
         outputs(0, (first,))
-        quantise_w2(second, 0, 256)
-        group_w2(third, 0, 128, nc.vector)
-        group_w2(third, 128, 256, nc.scalar)
+        hidden(last)
         quantise_w2(first, 256, N)
+        group_w2(second, 0, 256, W2S[2])
+        group_w2(third, 128, 256, W2S[5])
+        for t in range(1, 4):
+            outputs(t, (first,))
+        hidden_codes(last)
+        group_w2(third, 0, 128, W2S[4])
+        quantise_w2(second, 0, 256)
         quantise_w2(third, 0, 128)
-        outputs(1, (first,))
-        group_w2(last, 0, 128, nc.vector, True)
         outputs(0, (second, third))
-        quantise_w2(third, 128, 256)
-        quantise_w2(last, 0, 128)
-        group_w2(last, 128, 256, nc.scalar, True)
+        group_w2(last, 0, 128, W2S[6], True)
         quantise_w2(second, 256, N)
+        quantise_w2(last, 0, 128)
+        group_w2(last, 128, 256, W2S[7], True)
+        quantise_w2(third, 128, 256)
         outputs(0, (last,), nc.vector)
         outputs(1, (second, third))
+        group_w2(third, 256, N, W2S[8])
         fetch(0, 0)
         quantise_w2(last, 128, 256)
-        group_w2(third, 256, N, nc.scalar)
         outputs(1, (last,))
-        outputs(2, (first,))
+        group_w2(last, 256, N, W2S[9])
         fetch(0, 1)
         quantise_w2(third, 256, N)
-        group_w2(last, 256, N, nc.scalar)
         outputs(2, (second, third))
         outputs(3, (second, third))
         fetch(1, 0)
         quantise_w2(last, 256, N)
         outputs(2, (last,))
-        outputs(3, (last, first))
+        outputs(3, (last,))
+        if NADD < 1:
+            finish(0)
         fetch(1, 1)
-        turn_and_add(0)
-        turn_and_add(1)
-        turn_back(0)
-        turn_back(1)
-        store(0)
-        store(1)
+        for t in range(NADD):
+            turn_and_add(t)
+        for t in range(NADD):
+            turn_back(t)
+        for t in range(NADD):
+            store(t)
         fetch(2, 0)
+        if NADD < 2:
+            finish(1)
         fetch(2, 1)
         fetch(3, 0, 0, CUT)
         finish(2)

@@ -29,7 +29,7 @@ A = True
 S1 = 0
 S3 = 64
 W2S = (0, 128, 0, 128, 0, 128, 0, 128, 128, 128)
-NADD = 2
+NADD = 1
 N1 = 1
 NQ = 0
 EARLY = True

@@ -58,10 +58,6 @@ def tile_moe_rag_glu_sigmoid_kernel(tc, xT, w1, w3, w2, gate, offs, pos1, pos2, 
         pos1_sb = lists.tile([P, T // 16], U16, name="pos1_sb")
         pos2_sb = lists.tile([P, T // 16], U16, name="pos2_sb")
 
-        warm = keep.tile([P, 1], F32, name="warm")
-        nc.gpsimd.memset(warm[:], 0.0)
-        warm_out = keep.tile([P, 1], F32, name="warm_out")
-        nc.scalar.activation(out=warm_out[:], in_=warm[:], func=SIGMOID)
         x_scales = keep.tile([P, T], U8, name="x_scales", align_bytes=64)
         nc.gpsimd.memset(x_scales[:], 0)
 

@@ -253,7 +253,7 @@ def tile_moe_rag_glu_sigmoid_kernel(tc, xT, w1, w3, w2, gate, offs, pos1, pos2, 
         def store(t):
             total = s_tile([P, T], F32, f"total{t}")
             nc.scalar.copy(out=total[:], in_=summed[t][:].rearrange("p b i -> p (b i)"))
-            nc.sync.dma_start(out=out[t * P:(t + 1) * P, :], in_=total[:])
+            nc.scalar.dma_start(out=out[t * P:(t + 1) * P, :], in_=total[:])
 
         def ready(nm, e):
             quantise(nm, e)

@@ -68,22 +68,22 @@ def tile_moe_rag_glu_sigmoid_kernel(tc, xT, w1, w3, w2, gate, offs, pos1, pos2, 
         make_identity(nc, identity[:])
 
         w_raw, w2_raw = {}, {}
-        x_raw = keep.tile([P, 4, T], F32, name="x_raw")
+        x_raw = keep.tile([P, 4, T], F32, name="x_raw", align_bytes=256)
         load_rows(x_raw[:], xT)
         gate_cols = keep.tile([P, 2, 8], F32, name="gate_cols")
-        nc.sync.dma_start(out=gate_cols[:, :, 0:4], in_=gate[:, 0, :].rearrange("c (p j) -> p c j", j=4))
+        nc.scalar.dma_start(out=gate_cols[:, :, 0:4], in_=gate[:, 0, :].rearrange("c (p j) -> p c j", j=4))
         nc.sync.dma_start(offs_sb[:], offs)
         first, second, third, last = ORDER
 
         def load_w2(e, a, b):
-            raw = keep.tile([P, 4, b - a], F32, name=f"w2_raw{e}_{a}")
+            raw = keep.tile([P, 4, b - a], F32, name=f"w2_raw{e}_{a}", align_bytes=256)
             load_rows(raw[:], w2[e, :, a:b])
             for col in range(a, b, P):
                 w2_raw[e, col] = (raw, a)
 
         for i, e in enumerate(ORDER):
             for nm, w in (("w1", w1), ("w3", w3)):
-                w_raw[nm, e] = keep.tile([P, 4, H], F32, name=f"{nm}_raw{e}")
+                w_raw[nm, e] = keep.tile([P, 4, H], F32, name=f"{nm}_raw{e}", align_bytes=256)
                 load_rows(w_raw[nm, e][:], w[e])
             if e == second:
                 nc.sync.dma_start(pos1_sb[:], pos1)
@@ -93,8 +93,9 @@ def tile_moe_rag_glu_sigmoid_kernel(tc, xT, w1, w3, w2, gate, offs, pos1, pos2, 
         load_w2(third, 0, 256)
         load_w2(last, 0, 128)
         load_w2(last, 128, 256)
-        load_w2(third, 256, 512)
-        load_w2(last, 256, 512)
+        load_w2(third, 256, N)
+        load_w2(last, 256, 384)
+        load_w2(last, 384, N)
 
         gate_sb = {}
 
@@ -106,6 +107,8 @@ def tile_moe_rag_glu_sigmoid_kernel(tc, xT, w1, w3, w2, gate, offs, pos1, pos2, 
             nc.scalar.copy(out=gate_sb[c][:].rearrange("p (i b) -> p i b", b=4), in_=spread[:].rearrange("p b i -> p i b"))
 
 
+        warm = s_tile([P, 1], F32, "warm")
+        nc.scalar.activation(out=warm[:], in_=identity[:, 0:1], func=SIGMOID)
         xg = s_tile([P, T, 4], BF16, "xg")
         dst = xg[:].rearrange("p (c i) j -> p c j i", i=4)
         src = x_raw[:].rearrange("p j (c i) -> p c j i", i=4)
@@ -291,60 +294,61 @@ def tile_moe_rag_glu_sigmoid_kernel(tc, xT, w1, w3, w2, gate, offs, pos1, pos2, 
             if e != last:
                 hidden_codes(previous)
         ready("w3", last)
-        group_w2(first, 0, 256, W2S[0])
-        group_w2(first, 256, N, W2S[1])
-        group_w2(second, 256, N, W2S[3])
+        group_w2(first, 0, 256, 0)
+        group_w2(first, 256, N, 128)
         hidden_codes(third)
         quantise_w2(first, 0, 256)
         outputs(0, (first,))
+        outputs(1, (first,))
         hidden(last)
         quantise_w2(first, 256, N)
-        group_w2(second, 0, 256, W2S[2])
-        group_w2(third, 128, 256, W2S[5])
-        for t in range(1, 4):
-            outputs(t, (first,))
+        outputs(2, (first,))
+        outputs(3, (first,))
+        group_w2(second, 0, 256, 0)
         hidden_codes(last)
-        group_w2(third, 0, 128, W2S[4])
+        group_w2(second, 256, N, 0)
         quantise_w2(second, 0, 256)
+        group_w2(third, 0, 128, 0)
+        group_w2(third, 128, 256, 128)
+        quantise_w2(second, 256, N)
         quantise_w2(third, 0, 128)
         outputs(0, (second, third))
-        group_w2(last, 0, 128, W2S[6], True)
-        quantise_w2(second, 256, N)
-        quantise_w2(last, 0, 128)
-        group_w2(last, 128, 256, W2S[7], True)
+        group_w2(last, 0, 128, 0)
         quantise_w2(third, 128, 256)
-        outputs(0, (last,), nc.vector)
+        quantise_w2(last, 0, 128)
+        outputs(0, (last,))
         outputs(1, (second, third))
-        group_w2(third, 256, N, W2S[8])
-        fetch(0, 0)
+        group_w2(last, 128, 256, 0)
         quantise_w2(last, 128, 256)
+        fetch(0, 0)
+        group_w2(third, 256, 384, 128)
         outputs(1, (last,))
-        group_w2(last, 256, N, W2S[9])
+        group_w2(last, 256, 384, 128)
+        group_w2(third, 384, N, 128)
+        group_w2(last, 384, N, 128)
         fetch(0, 1)
-        quantise_w2(third, 256, N)
+        quantise_w2(third, 256, 384)
         outputs(2, (second, third))
-        outputs(3, (second, third))
+        turn_and_add(0)
         fetch(1, 0)
-        quantise_w2(last, 256, N)
+        quantise_w2(last, 256, 384)
         outputs(2, (last,))
+        quantise_w2(third, 384, N)
+        quantise_w2(last, 384, N)
+        outputs(3, (second, third))
         outputs(3, (last,))
-        if NADD < 1:
-            finish(0)
         fetch(1, 1)
-        for t in range(NADD):
-            turn_and_add(t)
-        for t in range(NADD):
-            turn_back(t)
-        for t in range(NADD):
-            store(t)
+        turn_and_add(1)
+        turn_back(0)
+        turn_back(1)
+        store(0)
+        store(1)
         fetch(2, 0)
-        if NADD < 2:
-            finish(1)
         fetch(2, 1)
         fetch(3, 0, 0, CUT)
         finish(2)
         fetch(3, 1, 0, CUT)
         fetch(3, 0, CUT, T)
-        finish(3, 0, CUT)
         fetch(3, 1, CUT, T)
+        finish(3, 0, CUT)
         finish(3, CUT, T)

@@ -21,8 +21,8 @@ P = 128
 FLOPS = 2 * S * (2 * K * H + H * N)
 
 ORDER = (1, 2, 3, 0)
-SH = (128, 112, 32, 128, 32, 128, 32, 80)
-CUT = 320
+SH = (128, 128, 48, 128, 48, 128, 48, 96)
+CUT = 256
 W2_ORDER = (2, 3, 1, 0)
 X_SHARE = 44
 A = True
@@ -303,14 +303,13 @@ def tile_moe_rag_glu_sigmoid_kernel(tc, xT, w1, w3, w2, gate, offs, pos1, pos2, 
         hidden(last)
         quantise_w2(first, 256, N)
         outputs(2, (first,))
-        outputs(3, (first,))
         group_w2(second, 0, 256, 0)
         hidden_codes(last)
-        group_w2(second, 256, N, 0)
+        group_w2(second, 256, N, 128)
+        outputs(3, (first,))
         quantise_w2(second, 0, 256)
         group_w2(third, 0, 128, 0)
-        group_w2(third, 128, 256, 128)
-        quantise_w2(second, 256, N)
+        group_w2(third, 128, 256, 0)
         quantise_w2(third, 0, 128)
         outputs(0, (second, third))
         group_w2(last, 0, 128, 0)
@@ -319,6 +318,7 @@ def tile_moe_rag_glu_sigmoid_kernel(tc, xT, w1, w3, w2, gate, offs, pos1, pos2, 
         outputs(0, (last,))
         outputs(1, (second, third))
         group_w2(last, 128, 256, 0)
+        quantise_w2(second, 256, N)
         quantise_w2(last, 128, 256)
         fetch(0, 0)
         group_w2(third, 256, 384, 128)

@@ -237,6 +237,12 @@ def tile_moe_rag_glu_sigmoid_kernel(tc, xT, w1, w3, w2, gate, offs, pos1, pos2, 
             nc.vector.tensor_tensor(out=total[:], in0=parts[t, 0, a][:], in1=parts[t, 1, a][:], op=ADD)
             nc.sync.dma_start(out=out[t * P:(t + 1) * P, a:b], in_=total[:])
 
+        def keep_warm(j):
+            codes, scales = wq["w3", last]
+            idle = psum.tile([P, 512], F32, name=f"idle{j}", tag="bank")
+            nc.tensor.matmul_mx(out=idle[:], lhsT=codes[:, 0:P].bitcast(FP8X4), lhsT_scale=scales[:, 0:P],
+                                rhs=codes[:].bitcast(FP8X4), rhs_scale=scales[:], start=True, stop=True)
+
         turned, summed = {}, {}
 
         def turn_and_add(t):
@@ -323,6 +329,9 @@ def tile_moe_rag_glu_sigmoid_kernel(tc, xT, w1, w3, w2, gate, offs, pos1, pos2, 
         fetch(0, 0)
         group_w2(third, 256, 384, 128)
         outputs(1, (last,))
+        keep_warm(20)
+        keep_warm(21)
+        keep_warm(22)
         group_w2(last, 256, 384, 128)
         group_w2(third, 384, N, 128)
         group_w2(last, 384, N, 128)
@@ -337,6 +346,8 @@ def tile_moe_rag_glu_sigmoid_kernel(tc, xT, w1, w3, w2, gate, offs, pos1, pos2, 
         quantise_w2(last, 384, N)
         outputs(3, (second, third))
         outputs(3, (last,))
+        keep_warm(40)
+        keep_warm(41)
         fetch(1, 1)
         turn_and_add(1)
         turn_back(0)

@@ -21,7 +21,7 @@ P = 128
 FLOPS = 2 * S * (2 * K * H + H * N)
 
 ORDER = (1, 2, 3, 0)
-SH = (128, 128, 48, 128, 48, 128, 48, 96)
+SH = (128, 128, 32, 128, 32, 128, 32, 80)
 CUT = 256
 W2_ORDER = (2, 3, 1, 0)
 X_SHARE = 44
@@ -138,7 +138,9 @@ def tile_moe_rag_glu_sigmoid_kernel(tc, xT, w1, w3, w2, gate, offs, pos1, pos2, 
             if share > 0:
                 nc.scalar.copy(out=dst[:, 0:share], in_=src[:, 0:share])
             if share < 128:
-                nc.vector.tensor_copy(out=dst[:, share:128], in_=src[:, share:128])
+                dst = wg[:].rearrange("p (u v) m j -> p u m j v", v=2)
+                src = w_raw[nm, e][:].rearrange("p j (m u v) -> p u m j v", u=2, v=2)
+                nc.vector.tensor_copy(out=dst[:, :, share:128], in_=src[:, :, share:128])
             grouped[nm, e] = wg
 
         def quantise(nm, e):

@@ -21,20 +21,12 @@ P = 128
 FLOPS = 2 * S * (2 * K * H + H * N)
 
 ORDER = (1, 2, 3, 0)
-SH = (128, 128, 32, 128, 32, 128, 32, 80)
-CUT = 256
-W2_ORDER = (2, 3, 1, 0)
-X_SHARE = 44
-A = True
-S1 = 0
-S3 = 64
-W2S = (0, 128, 0, 128, 0, 128, 0, 128, 128, 128)
-NADD = 1
-N1 = 1
-NQ = 0
-EARLY = True
-Q10 = True
-LAST_SHARE = 40
+X_PIECES = ((0, 512),)
+X_ON_SCALAR = 176
+IN_HALVES = ()
+W2_PIECES = ((0, 0, 512), (1, 0, 512), (2, 0, 256), (3, 0, 128), (3, 128, 256), (2, 256, 512), (3, 256, 384), (3, 384, 512))
+W1_ON_SCALAR = (128, 24, 32, 40)
+W3_ON_SCALAR = (128, 120, 104, 88)
 ON_SCALAR_BUFS = 11
 ON_VECTOR_BUFS = 34
 
@@ -48,11 +40,19 @@ def tile_moe_rag_glu_sigmoid_kernel(tc, xT, w1, w3, w2, gate, offs, pos1, pos2, 
         by_vector = ctx.enter_context(tc.tile_pool(name="by_vector", bufs=ON_VECTOR_BUFS))
         psum = ctx.enter_context(tc.psum_pool(name="psum", bufs=8))
 
-        def s_tile(shape, dtype, name):
-            return by_scalar.tile(shape, dtype, name=name, tag="s", align_bytes=64)
-
-        def v_tile(shape, dtype, name):
+        def made_by(engine, shape, dtype, name):
+            if engine is nc.scalar:
+                return by_scalar.tile(shape, dtype, name=name, tag="s", align_bytes=64)
             return by_vector.tile(shape, dtype, name=name, tag="v", align_bytes=64)
+
+        def copy(engine, dst, src):
+            if engine is nc.scalar:
+                nc.scalar.copy(out=dst, in_=src)
+            else:
+                nc.vector.tensor_copy(out=dst, in_=src)
+
+        def bank(shape, name):
+            return psum.tile(shape, F32, name=name, tag="bank")
 
         offs_sb = lists.tile([P, S // 16], U16, name="offs_sb")
         pos1_sb = lists.tile([P, T // 16], U16, name="pos1_sb")
@@ -60,296 +60,258 @@ def tile_moe_rag_glu_sigmoid_kernel(tc, xT, w1, w3, w2, gate, offs, pos1, pos2, 
 
         x_scales = keep.tile([P, T], U8, name="x_scales", align_bytes=64)
         nc.gpsimd.memset(x_scales[:], 0)
-
-        def load_rows(dst, src):
-            nc.sync.dma_start(out=dst, in_=src.rearrange("(p j) c -> p j c", j=4))
-
         identity = keep.tile([P, P], F32, name="identity")
         make_identity(nc, identity[:])
 
-        w_raw, w2_raw = {}, {}
-        x_raw = keep.tile([P, 4, T], F32, name="x_raw", align_bytes=256)
-        load_rows(x_raw[:], xT)
+        def load_rows(src, name):
+            raw = keep.tile([P, 4, src.shape[1]], F32, name=name, align_bytes=256)
+            nc.sync.dma_start(out=raw[:], in_=src.rearrange("(p j) c -> p j c", j=4))
+            return raw
+
+        first, second, third, last = ORDER
+        x_raw = [load_rows(xT[:, a:b], f"x_raw{a}") for a, b in X_PIECES]
         gate_cols = keep.tile([P, 2, 8], F32, name="gate_cols")
         nc.scalar.dma_start(out=gate_cols[:, :, 0:4], in_=gate[:, 0, :].rearrange("c (p j) -> p c j", j=4))
         nc.sync.dma_start(offs_sb[:], offs)
-        first, second, third, last = ORDER
-
-        def load_w2(e, a, b):
-            raw = keep.tile([P, 4, b - a], F32, name=f"w2_raw{e}_{a}", align_bytes=256)
-            load_rows(raw[:], w2[e, :, a:b])
-            for col in range(a, b, P):
-                w2_raw[e, col] = (raw, a)
-
-        for i, e in enumerate(ORDER):
+        w_raw, w2_raw = {}, {}
+        for e in ORDER:
             for nm, w in (("w1", w1), ("w3", w3)):
-                w_raw[nm, e] = keep.tile([P, 4, H], F32, name=f"{nm}_raw{e}", align_bytes=256)
-                load_rows(w_raw[nm, e][:], w[e])
+                width = H // 2 if (nm, e) in IN_HALVES else H
+                w_raw[nm, e] = [load_rows(w[e, :, a:a + width], f"{nm}_raw{e}_{a}") for a in range(0, H, width)]
             if e == second:
                 nc.sync.dma_start(pos1_sb[:], pos1)
                 nc.sync.dma_start(pos2_sb[:], pos2)
-        load_w2(first, 0, N)
-        load_w2(second, 0, N)
-        load_w2(third, 0, 256)
-        load_w2(last, 0, 128)
-        load_w2(last, 128, 256)
-        load_w2(third, 256, N)
-        load_w2(last, 256, 384)
-        load_w2(last, 384, N)
+        for i, a, b in W2_PIECES:
+            e = ORDER[i]
+            raw = load_rows(w2[e, :, a:b], f"w2_raw{e}_{a}")
+            for col in range(a, b, P):
+                w2_raw[e, col] = (raw, a)
 
-        gate_sb = {}
-
-        def spread_gate(c):
-            spread = psum.tile([P, 4, P], F32, name=f"spread{c}", tag="bank")
-            for b in range(4):
-                nc.tensor.transpose(spread[:, b, :], gate_cols[:, c, b:b + 1].to_broadcast([P, P]), identity[:])
-            gate_sb[c] = s_tile([P, T], F32, f"gate_sb{c}")
-            nc.scalar.copy(out=gate_sb[c][:].rearrange("p (i b) -> p i b", b=4), in_=spread[:].rearrange("p b i -> p i b"))
-
-
-        warm = s_tile([P, 1], F32, "warm")
+        warm = made_by(nc.scalar, [P, 1], F32, "warm")
         nc.scalar.activation(out=warm[:], in_=identity[:, 0:1], func=SIGMOID)
-        xg = s_tile([P, T, 4], BF16, "xg")
-        dst = xg[:].rearrange("p (c i) j -> p c j i", i=4)
-        src = x_raw[:].rearrange("p j (c i) -> p c j i", i=4)
-        nc.scalar.copy(out=dst[:, 0:X_SHARE], in_=src[:, 0:X_SHARE])
-        nc.vector.tensor_copy(out=dst[:, X_SHARE:128], in_=src[:, X_SHARE:128])
-        spread_gate(0)
-        spread_gate(1)
-        x_words = v_tile([P, T], U32, "x_words")
-        nc.vector.quantize_mx(out=x_words[:].bitcast(FP8X4), scales=x_scales[:], in_=xg[:].rearrange("p c j -> p (c j)"))
 
-        g_codes, g_scales = {}, {}
+        gate_rows = {}
 
-        def gather(e):
+        def spread_gate(c, engine):
+            spread = bank([P, 4, P], f"spread{c}")
+            for j in range(4):
+                nc.tensor.transpose(spread[:, j, :], gate_cols[:, c, j:j + 1].to_broadcast([P, P]), identity[:])
+            gate_rows[c] = made_by(engine, [P, T], F32, f"gate_rows{c}")
+            copy(engine, gate_rows[c][:].rearrange("p (i j) -> p i j", j=4), spread[:].rearrange("p j i -> p i j"))
+
+
+        def interleave(engine, grouped, raw):
+            copy(engine, grouped.rearrange("p (c i) j -> p c j i", i=4), raw.rearrange("p j (c i) -> p c j i", i=4))
+
+        x_words = made_by(nc.vector, [P, T], U32, "x_words")
+        x_grouped = []
+        for raw, (a, b) in zip(x_raw, X_PIECES):
+            share = X_ON_SCALAR if b == T else 0
+            x_grouped.append(made_by(nc.scalar if share else nc.vector, [P, b - a, 4], BF16, f"x_grouped{a}"))
+            if share:
+                interleave(nc.scalar, x_grouped[-1][:, 0:share, :], raw[:, :, 0:share])
+            interleave(nc.vector, x_grouped[-1][:, share:b - a, :], raw[:, :, share:b - a])
+            if b == T:
+                spread_gate(0, nc.scalar)
+                spread_gate(1, nc.scalar)
+            nc.vector.quantize_mx(out=x_words[:, a:b].bitcast(FP8X4), scales=x_scales[:, a:b],
+                                  in_=x_grouped[-1][:].rearrange("p c j -> p (c j)"))
+
+        slot_words, slot_scales = {}, {}
+
+        def gather_tokens(e):
             a, b = STARTS[e], STARTS[e + 1]
             idx = offs_sb[:, a // 16:b // 16]
-            g_codes[e] = v_tile([P, b - a], U32, f"g_codes{e}")
-            nc.vector.tensor_copy(out=g_codes[e][:], in_=x_words[:].indirect(idx))
-            g_scales[e] = v_tile([P, b - a], U8, f"g_scales{e}")
-            nc.vector.tensor_copy(out=g_scales[e][:], in_=x_scales[:].indirect(idx))
+            slot_words[e] = made_by(nc.vector, [P, b - a], U32, f"slot_words{e}")
+            nc.vector.tensor_copy(out=slot_words[e][:], in_=x_words[:].indirect(idx))
+            slot_scales[e] = made_by(nc.vector, [P, b - a], U8, f"slot_scales{e}")
+            nc.vector.tensor_copy(out=slot_scales[e][:], in_=x_scales[:].indirect(idx))
 
-        grouped, wq = {}, {}
+        grouped = {}
 
-        def group(nm, e, share):
-            wg = s_tile([P, 4, 128, 4], BF16, f"g{nm}{e}")
-            dst = wg[:].rearrange("p t m j -> p m j t")
-            src = w_raw[nm, e][:].rearrange("p j (m t) -> p m j t", t=4)
-            if share > 0:
-                nc.scalar.copy(out=dst[:, 0:share], in_=src[:, 0:share])
-            if share < 128:
-                dst = wg[:].rearrange("p (u v) m j -> p u m j v", v=2)
-                src = w_raw[nm, e][:].rearrange("p j (m u v) -> p u m j v", u=2, v=2)
-                nc.vector.tensor_copy(out=dst[:, :, share:128], in_=src[:, :, share:128])
-            grouped[nm, e] = wg
+        def regroup(nm, e, share):
+            grouped[nm, e] = made_by(nc.scalar, [P, 4, P, 4], BF16, f"g{nm}{e}")
+            width = P // len(w_raw[nm, e])
+            for k, raw in enumerate(w_raw[nm, e]):
+                cut = min(max(share - k * width, 0), width)
+                piece = grouped[nm, e][:, :, k * width:(k + 1) * width, :]
+                if cut > 0:
+                    nc.scalar.copy(out=piece.rearrange("p t m j -> p m j t")[:, 0:cut],
+                                   in_=raw[:].rearrange("p j (m t) -> p m j t", t=4)[:, 0:cut])
+                if cut < width:
+                    nc.vector.tensor_copy(out=piece.rearrange("p (u v) m j -> p u m j v", v=2)[:, :, cut:width],
+                                          in_=raw[:].rearrange("p j (m u v) -> p u m j v", u=2, v=2)[:, :, cut:width])
 
-        def quantise(nm, e):
-            codes = v_tile([P, 512], U32, f"q{nm}{e}")
-            scales = keep.tile([P, 512], U8, name=f"{nm}_scales{e}", align_bytes=64)
-            nc.vector.quantize_mx(out=codes[:].bitcast(FP8X4), scales=scales[:],
-                                  in_=grouped[nm, e][:].rearrange("p t m j -> p (t m j)"))
-            wq[nm, e] = (codes, scales)
+        def quantise(source, name):
+            width = source.shape[1] // 4
+            codes = made_by(nc.vector, [P, width], U32, f"q{name}")
+            scales = keep.tile([P, width], U8, name=f"scales{name}", align_bytes=64)
+            nc.vector.quantize_mx(out=codes[:].bitcast(FP8X4), scales=scales[:], in_=source)
+            return codes, scales
 
         def chunks(e):
             return range(STARTS[e] // P, STARTS[e + 1] // P)
 
-        banks, sigs, h_bf, h_codes = {}, {}, {}, {}
-        h_scales = {}
+        sums, sigs, hidden, h_codes = {}, {}, {}, {}
 
         def products(nm, e):
-            codes, scales = wq[nm, e]
+            codes, scales = quantise(grouped[nm, e][:].rearrange("p t m j -> p (t m j)"), f"{nm}{e}")
             for chunk in chunks(e):
                 slots = slice(chunk * P - STARTS[e], (chunk + 1) * P - STARTS[e])
-                acc = psum.tile([P, 4, P], F32, name=f"p{nm}{chunk}", tag="bank")
+                sums[nm, chunk] = bank([P, 4, P], f"p{nm}{chunk}")
                 for t in range(4):
                     cols = slice(t * P, (t + 1) * P)
-                    nc.tensor.matmul_mx(out=acc[:, t, :],
+                    nc.tensor.matmul_mx(out=sums[nm, chunk][:, t, :],
                                         lhsT=codes[:, cols].bitcast(FP8X4), lhsT_scale=scales[:, cols],
-                                        rhs=g_codes[e][:, slots].bitcast(FP8X4), rhs_scale=g_scales[e][:, slots],
+                                        rhs=slot_words[e][:, slots].bitcast(FP8X4), rhs_scale=slot_scales[e][:, slots],
                                         start=True, stop=True)
-                banks[nm, chunk] = acc
 
         def sigmoids(e):
             for chunk in chunks(e):
-                sigs[chunk] = s_tile([P, P, 4], F32, f"sig{chunk}")
-                nc.scalar.activation(out=sigs[chunk][:], in_=banks["w1", chunk][:].rearrange("p t n -> p n t"), func=SIGMOID)
+                sigs[chunk] = made_by(nc.scalar, [P, P, 4], F32, f"sig{chunk}")
+                nc.scalar.activation(out=sigs[chunk][:], in_=sums["w1", chunk][:].rearrange("p t n -> p n t"), func=SIGMOID)
 
         def gated(chunk):
-            h_bf[chunk] = v_tile([P, P, 4], BF16, f"h_bf{chunk}")
-            nc.vector.tensor_tensor(out=h_bf[chunk][:], in0=banks["w3", chunk][:].rearrange("p t n -> p n t"), in1=sigs[chunk][:], op=MULT)
+            hidden[chunk] = made_by(nc.vector, [P, P, 4], BF16, f"hidden{chunk}")
+            nc.vector.tensor_tensor(out=hidden[chunk][:], in0=sums["w3", chunk][:].rearrange("p t n -> p n t"), in1=sigs[chunk][:], op=MULT)
 
-        def quantise_h(chunk):
-            h_codes[chunk] = v_tile([P, P], U32, f"hq{chunk}")
-            h_scales[chunk] = keep.tile([P, P], U8, name=f"h_scales{chunk}", align_bytes=64)
-            nc.vector.quantize_mx(out=h_codes[chunk][:].bitcast(FP8X4), scales=h_scales[chunk][:],
-                                  in_=h_bf[chunk][:].rearrange("p n t -> p (n t)"))
+        def quantise_hidden(e):
+            for chunk in chunks(e):
+                h_codes[chunk] = quantise(hidden[chunk][:].rearrange("p n t -> p (n t)"), f"h{chunk}")
 
-        w2g, w2q = {}, {}
+        w2_grouped, w2_codes = {}, {}
 
-        def group_w2(e, a, b, share, shared=False):
-            if shared:
-                wg = keep.tile([P, b - a, 4], BF16, name=f"gw2{e}_{a}", tag="shared", align_bytes=64)
-            else:
-                wg = (s_tile if share else v_tile)([P, b - a, 4], BF16, f"gw2{e}_{a}")
+        def regroup_w2(e, a, b, engine):
+            w2_grouped[e, a] = made_by(engine, [P, b - a, 4], BF16, f"gw2{e}_{a}")
             raw, start = w2_raw[e, a]
-            dst = wg[:].rearrange("p (c i) j -> p c j i", i=4)
-            src = raw[:, :, a - start:b - start].rearrange("p j (c i) -> p c j i", i=4)
-            h = (b - a) // 4 * share // 128
-            if h > 0:
-                nc.scalar.copy(out=dst[:, 0:h], in_=src[:, 0:h])
-            if h < (b - a) // 4:
-                nc.vector.tensor_copy(out=dst[:, h:], in_=src[:, h:])
-            w2g[e, a] = wg
+            interleave(engine, w2_grouped[e, a][:], raw[:, :, a - start:b - start])
 
         def quantise_w2(e, a, b):
-            codes = v_tile([P, b - a], U32, f"qw2{e}_{a}")
-            scales = keep.tile([P, b - a], U8, name=f"w2_scales{e}_{a}", align_bytes=64)
-            nc.vector.quantize_mx(out=codes[:].bitcast(FP8X4), scales=scales[:],
-                                  in_=w2g[e, a][:].rearrange("p c j -> p (c j)"))
+            codes, scales = quantise(w2_grouped[e, a][:].rearrange("p c j -> p (c j)"), f"w2{e}_{a}")
             for col in range(a, b, P):
-                w2q[col // P, e] = (codes[:, col - a:col - a + P], scales[:, col - a:col - a + P])
+                w2_codes[col // P, e] = (codes[:, col - a:col - a + P], scales[:, col - a:col - a + P])
 
-        ys, parts = {}, {}
+        ys, y_sums = {}, {}
 
-        def outputs(t, experts, engine=nc.scalar):
-            if t not in ys:
-                ys[t] = s_tile([P, S], F32, f"y{t}")
+        def multiply_w2(t, experts):
             a, b = STARTS[experts[0]], STARTS[experts[-1] + 1]
-            py = psum.tile([P, b - a], F32, name=f"py{t}{experts[0]}", tag="bank")
+            py = bank([P, b - a], f"py{t}{experts[0]}")
             for e in experts:
-                codes, scales = w2q[t, e]
+                codes, scales = w2_codes[t, e]
                 for chunk in chunks(e):
                     place = chunk * P - a
                     nc.tensor.matmul_mx(out=py[:, place:place + P],
                                         lhsT=codes.bitcast(FP8X4), lhsT_scale=scales,
-                                        rhs=h_codes[chunk][:].bitcast(FP8X4), rhs_scale=h_scales[chunk][:],
+                                        rhs=h_codes[chunk][0][:].bitcast(FP8X4), rhs_scale=h_codes[chunk][1][:],
                                         start=True, stop=True)
-            if engine is nc.scalar:
-                nc.scalar.copy(out=ys[t][:, a:b], in_=py[:])
-            else:
-                nc.vector.tensor_copy(out=ys[t][:, a:b], in_=py[:])
+            y_sums[t, experts] = py
+
+        def bring(t, experts, engine):
+            if t not in ys:
+                ys[t] = made_by(nc.scalar, [P, S], F32, f"y{t}")
+            copy(engine, ys[t][:, STARTS[experts[0]]:STARTS[experts[-1] + 1]], y_sums[t, experts][:])
+
+        def outputs(t, experts, engine):
+            multiply_w2(t, experts)
+            bring(t, experts, engine)
+
+        parts, turned = {}, {}
 
         def fetch(t, c, a=0, b=T):
-            parts[t, c, a] = v_tile([P, b - a], F32, f"r{t}{c}{a}")
+            parts[t, c, a] = made_by(nc.vector, [P, b - a], F32, f"part{t}{c}_{a}")
             idx = (pos1_sb, pos2_sb)[c][:, a // 16:b // 16]
-            nc.vector.tensor_tensor(out=parts[t, c, a][:], in0=ys[t][:].indirect(idx), in1=gate_sb[c][:, a:b], op=MULT)
-
-        def finish(t, a=0, b=T):
-            total = v_tile([P, b - a], F32, f"sum{t}{a}")
-            nc.vector.tensor_tensor(out=total[:], in0=parts[t, 0, a][:], in1=parts[t, 1, a][:], op=ADD)
-            nc.sync.dma_start(out=out[t * P:(t + 1) * P, a:b], in_=total[:])
-
-        def keep_warm(j):
-            codes, scales = wq["w3", last]
-            idle = psum.tile([P, 512], F32, name=f"idle{j}", tag="bank")
-            nc.tensor.matmul_mx(out=idle[:], lhsT=codes[:, 0:P].bitcast(FP8X4), lhsT_scale=scales[:, 0:P],
-                                rhs=codes[:].bitcast(FP8X4), rhs_scale=scales[:], start=True, stop=True)
-
-        turned, summed = {}, {}
+            nc.vector.tensor_tensor(out=parts[t, c, a][:], in0=ys[t][:].indirect(idx), in1=gate_rows[c][:, a:b], op=MULT)
 
         def turn_and_add(t):
-            turned[t] = psum.tile([P, 4, P], F32, name=f"turned{t}", tag="bank")
+            turned[t] = bank([P, 4, P], f"turned{t}")
             for b in range(4):
+                cols = slice(b * P, (b + 1) * P)
                 for c in range(2):
-                    nc.tensor.matmul(out=turned[t][:, b, :], lhsT=parts[t, c, 0][:, b * P:(b + 1) * P], rhs=identity[:],
+                    nc.tensor.matmul(out=turned[t][:, b, :], lhsT=parts[t, c, 0][:, cols], rhs=identity[:],
                                      start=(c == 0), stop=(c == 1), is_transpose=True)
 
         def turn_back(t):
-            by_token = s_tile([P, 4, P], F32, f"by_token{t}")
+            by_token = made_by(nc.scalar, [P, 4, P], F32, f"by_token{t}")
             nc.scalar.copy(out=by_token[:], in_=turned[t][:])
-            summed[t] = psum.tile([P, 4, P], F32, name=f"summed{t}", tag="bank")
+            turned[t] = bank([P, 4, P], f"summed{t}")
             for b in range(4):
-                nc.tensor.transpose(summed[t][:, b, :], by_token[:, b, :], identity[:])
+                nc.tensor.transpose(turned[t][:, b, :], by_token[:, b, :], identity[:])
 
         def store(t):
-            total = s_tile([P, T], F32, f"total{t}")
-            nc.scalar.copy(out=total[:], in_=summed[t][:].rearrange("p b i -> p (b i)"))
+            total = made_by(nc.scalar, [P, T], F32, f"total{t}")
+            nc.scalar.copy(out=total[:], in_=turned[t][:].rearrange("p b i -> p (b i)"))
             nc.scalar.dma_start(out=out[t * P:(t + 1) * P, :], in_=total[:])
 
-        def ready(nm, e):
-            quantise(nm, e)
-            products(nm, e)
+        def finish(t, a=0, b=T):
+            total = made_by(nc.vector, [P, b - a], F32, f"total{t}_{a}")
+            nc.vector.tensor_tensor(out=total[:], in0=parts[t, 0, a][:], in1=parts[t, 1, a][:], op=ADD)
+            nc.sync.dma_start(out=out[t * P:(t + 1) * P, a:b], in_=total[:])
 
-        def hidden(e):
-            for chunk in chunks(e):
-                gated(chunk)
-
-        def hidden_codes(e):
-            for chunk in chunks(e):
-                quantise_h(chunk)
-
-        eng = {"S": nc.scalar, "V": nc.vector}
-        gather(first)
-        gather(second)
-        group("w1", first, SH[0])
-        ready("w1", first)
-        gather(third)
-        group("w3", first, SH[1])
+        SC, VE = nc.scalar, nc.vector
+        gather_tokens(first)
+        gather_tokens(second)
+        regroup("w1", first, W1_ON_SCALAR[0])
+        products("w1", first)
+        gather_tokens(third)
+        gather_tokens(last)
+        regroup("w3", first, W3_ON_SCALAR[0])
         sigmoids(first)
         for i in range(1, E):
             previous, e = ORDER[i - 1], ORDER[i]
-            ready("w3", previous)
-            group("w1", e, SH[2 * i])
-            if e == second:
-                gather(last)
-            for chunk in chunks(previous)[:N1]:
-                gated(chunk)
-            ready("w1", e)
-            group("w3", e, SH[2 * i + 1])
+            products("w3", previous)
+            regroup("w1", e, W1_ON_SCALAR[i])
+            gated(chunks(previous)[0])
+            products("w1", e)
+            regroup("w3", e, W3_ON_SCALAR[i])
             sigmoids(e)
-            for chunk in chunks(previous)[N1:]:
+            for chunk in chunks(previous)[1:]:
                 gated(chunk)
-            if e != last:
-                hidden_codes(previous)
-        ready("w3", last)
-        group_w2(first, 0, 256, 0)
-        group_w2(first, 256, N, 128)
-        hidden_codes(third)
+            quantise_hidden(previous)
+        products("w3", last)
+        regroup_w2(first, 256, N, SC)
+        regroup_w2(first, 0, 256, VE)
+        gated(chunks(last)[0])
         quantise_w2(first, 0, 256)
-        outputs(0, (first,))
-        outputs(1, (first,))
-        hidden(last)
+        multiply_w2(0, (first,))
+        multiply_w2(1, (first,))
+        quantise_hidden(last)
+        regroup_w2(second, 256, N, SC)
+        regroup_w2(second, 0, 256, VE)
         quantise_w2(first, 256, N)
-        outputs(2, (first,))
-        group_w2(second, 0, 256, 0)
-        hidden_codes(last)
-        group_w2(second, 256, N, 128)
-        outputs(3, (first,))
+        bring(0, (first,), SC)
+        bring(1, (first,), SC)
+        outputs(2, (first,), SC)
+        outputs(3, (first,), SC)
         quantise_w2(second, 0, 256)
-        group_w2(third, 0, 128, 0)
-        group_w2(third, 128, 256, 0)
+        regroup_w2(third, 0, 128, VE)
+        regroup_w2(third, 128, 256, VE)
         quantise_w2(third, 0, 128)
-        outputs(0, (second, third))
-        group_w2(last, 0, 128, 0)
+        outputs(0, (second, third), SC)
+        regroup_w2(last, 0, 128, VE)
         quantise_w2(third, 128, 256)
         quantise_w2(last, 0, 128)
-        outputs(0, (last,))
-        outputs(1, (second, third))
-        group_w2(last, 128, 256, 0)
+        outputs(0, (last,), SC)
+        outputs(1, (second, third), SC)
+        regroup_w2(last, 128, 256, VE)
         quantise_w2(second, 256, N)
         quantise_w2(last, 128, 256)
         fetch(0, 0)
-        group_w2(third, 256, 384, 128)
-        outputs(1, (last,))
-        keep_warm(20)
-        keep_warm(21)
-        keep_warm(22)
-        group_w2(last, 256, 384, 128)
-        group_w2(third, 384, N, 128)
-        group_w2(last, 384, N, 128)
+        regroup_w2(third, 256, 384, SC)
+        outputs(1, (last,), SC)
+        regroup_w2(last, 256, 384, SC)
+        regroup_w2(third, 384, N, SC)
+        regroup_w2(last, 384, N, SC)
         fetch(0, 1)
         quantise_w2(third, 256, 384)
-        outputs(2, (second, third))
-        turn_and_add(0)
+        outputs(2, (second, third), SC)
         fetch(1, 0)
         quantise_w2(last, 256, 384)
-        outputs(2, (last,))
+        outputs(2, (last,), SC)
         quantise_w2(third, 384, N)
         quantise_w2(last, 384, N)
-        outputs(3, (second, third))
-        outputs(3, (last,))
-        keep_warm(40)
-        keep_warm(41)
+        outputs(3, (second, third), SC)
+        outputs(3, (last,), SC)
+        turn_and_add(0)
         fetch(1, 1)
         turn_and_add(1)
         turn_back(0)
@@ -358,10 +320,10 @@ def tile_moe_rag_glu_sigmoid_kernel(tc, xT, w1, w3, w2, gate, offs, pos1, pos2, 
         store(1)
         fetch(2, 0)
         fetch(2, 1)
-        fetch(3, 0, 0, CUT)
+        fetch(3, 0, 0, 256)
         finish(2)
-        fetch(3, 1, 0, CUT)
-        fetch(3, 0, CUT, T)
-        fetch(3, 1, CUT, T)
-        finish(3, 0, CUT)
-        finish(3, CUT, T)
+        fetch(3, 1, 0, 256)
+        fetch(3, 0, 256, T)
+        fetch(3, 1, 256, T)
+        finish(3, 0, 256)
+        finish(3, 256, T)

@@ -24,9 +24,10 @@ ORDER = (1, 2, 3, 0)
 X_PIECES = ((0, 512),)
 X_ON_SCALAR = 176
 IN_HALVES = ()
-W2_PIECES = ((0, 0, 512), (1, 0, 512), (2, 0, 256), (3, 0, 128), (3, 128, 256), (2, 256, 512), (3, 256, 384), (3, 384, 512))
-W1_ON_SCALAR = (128, 24, 32, 40)
-W3_ON_SCALAR = (128, 120, 104, 88)
+W2_PIECES = ((0, 0, 512), (1, 0, 128), (2, 0, 128), (3, 0, 128), (1, 128, 256), (2, 128, 256), (3, 128, 256),
+             (1, 256, 512), (2, 256, 512), (3, 256, 384), (3, 384, 512))
+W1_ON_SCALAR = (128, 32, 32, 40)
+W3_ON_SCALAR = (128, 128, 128, 88)
 ON_SCALAR_BUFS = 11
 ON_VECTOR_BUFS = 34
 
@@ -233,9 +234,12 @@ def tile_moe_rag_glu_sigmoid_kernel(tc, xT, w1, w3, w2, gate, offs, pos1, pos2, 
         def turn_back(t):
             by_token = made_by(nc.scalar, [P, 4, P], F32, f"by_token{t}")
             nc.scalar.copy(out=by_token[:], in_=turned[t][:])
+            parts[t] = by_token
+
+        def turn_again(t):
             turned[t] = bank([P, 4, P], f"summed{t}")
             for b in range(4):
-                nc.tensor.transpose(turned[t][:, b, :], by_token[:, b, :], identity[:])
+                nc.tensor.transpose(turned[t][:, b, :], parts[t][:, b, :], identity[:])
 
         def store(t):
             total = made_by(nc.scalar, [P, T], F32, f"total{t}")
@@ -268,57 +272,77 @@ def tile_moe_rag_glu_sigmoid_kernel(tc, xT, w1, w3, w2, gate, offs, pos1, pos2, 
                 gated(chunk)
             quantise_hidden(previous)
         products("w3", last)
-        regroup_w2(first, 256, N, SC)
-        regroup_w2(first, 0, 256, VE)
-        gated(chunks(last)[0])
-        quantise_w2(first, 0, 256)
+        regroup_w2(first, 0, 128, SC)
+        regroup_w2(second, 0, 128, VE)
+        regroup_w2(third, 0, 128, SC)
+        regroup_w2(last, 0, 128, SC)
+        quantise_w2(first, 0, 128)
         multiply_w2(0, (first,))
-        multiply_w2(1, (first,))
-        quantise_hidden(last)
-        regroup_w2(second, 256, N, SC)
-        regroup_w2(second, 0, 256, VE)
-        quantise_w2(first, 256, N)
-        bring(0, (first,), SC)
-        bring(1, (first,), SC)
-        outputs(2, (first,), SC)
-        outputs(3, (first,), SC)
-        quantise_w2(second, 0, 256)
-        regroup_w2(third, 0, 128, VE)
-        regroup_w2(third, 128, 256, VE)
+        quantise_w2(second, 0, 128)
         quantise_w2(third, 0, 128)
-        outputs(0, (second, third), SC)
-        regroup_w2(last, 0, 128, VE)
-        quantise_w2(third, 128, 256)
+        multiply_w2(0, (second, third))
+        regroup_w2(first, 128, 256, SC)
+        regroup_w2(first, 256, 384, SC)
+        gated(chunks(last)[0])
         quantise_w2(last, 0, 128)
-        outputs(0, (last,), SC)
-        outputs(1, (second, third), SC)
-        regroup_w2(last, 128, 256, VE)
-        quantise_w2(second, 256, N)
+        quantise_hidden(last)
+        multiply_w2(0, (last,))
+        bring(0, (first,), SC)
+        regroup_w2(second, 128, 256, VE)
+        regroup_w2(third, 128, 256, VE)
+        regroup_w2(last, 128, 256, SC)
+        bring(0, (second, third), SC)
+        bring(0, (last,), SC)
+        quantise_w2(first, 128, 256)
+        multiply_w2(1, (first,))
+        quantise_w2(second, 128, 256)
+        quantise_w2(third, 128, 256)
+        multiply_w2(1, (second, third))
         quantise_w2(last, 128, 256)
+        multiply_w2(1, (last,))
         fetch(0, 0)
-        regroup_w2(third, 256, 384, SC)
-        outputs(1, (last,), SC)
-        regroup_w2(last, 256, 384, SC)
-        regroup_w2(third, 384, N, SC)
-        regroup_w2(last, 384, N, SC)
+        bring(1, (first,), SC)
+        regroup_w2(second, 256, 384, SC)
+        bring(1, (second, third), SC)
+        bring(1, (last,), SC)
+        quantise_w2(first, 256, 384)
         fetch(0, 1)
-        quantise_w2(third, 256, 384)
-        outputs(2, (second, third), SC)
-        fetch(1, 0)
-        quantise_w2(last, 256, 384)
-        outputs(2, (last,), SC)
-        quantise_w2(third, 384, N)
-        quantise_w2(last, 384, N)
-        outputs(3, (second, third), SC)
-        outputs(3, (last,), SC)
         turn_and_add(0)
+        regroup_w2(third, 256, 384, SC)
+        regroup_w2(last, 256, 384, SC)
+        regroup_w2(first, 384, N, SC)
+        fetch(1, 0)
+        quantise_w2(second, 256, 384)
+        quantise_w2(third, 256, 384)
+        multiply_w2(2, (first,))
+        multiply_w2(2, (second, third))
+        quantise_w2(last, 256, 384)
+        multiply_w2(2, (last,))
+        regroup_w2(second, 384, N, SC)
+        bring(2, (first,), SC)
+        bring(2, (second, third), SC)
+        bring(2, (last,), SC)
         fetch(1, 1)
+        quantise_w2(first, 384, N)
+        multiply_w2(3, (first,))
+        regroup_w2(third, 384, N, VE)
+        regroup_w2(last, 384, N, VE)
+        quantise_w2(second, 384, N)
+        quantise_w2(third, 384, N)
+        multiply_w2(3, (second, third))
+        quantise_w2(last, 384, N)
+        multiply_w2(3, (last,))
+        fetch(2, 0)
         turn_and_add(1)
         turn_back(0)
+        bring(3, (first,), SC)
+        bring(3, (second, third), SC)
+        bring(3, (last,), SC)
+        turn_again(0)
         turn_back(1)
+        turn_again(1)
         store(0)
         store(1)
-        fetch(2, 0)
         fetch(2, 1)
         fetch(3, 0, 0, 256)
         finish(2)

@@ -27,7 +27,7 @@ IN_HALVES = ()
 W2_PIECES = ((0, 0, 512), (1, 0, 128), (2, 0, 128), (3, 0, 128), (1, 128, 256), (2, 128, 256), (3, 128, 256),
              (1, 256, 512), (2, 256, 512), (3, 256, 384), (3, 384, 512))
 W1_ON_SCALAR = (128, 32, 32, 40)
-W3_ON_SCALAR = (128, 128, 128, 88)
+W3_ON_SCALAR = (128, 128, 112, 80)
 ON_SCALAR_BUFS = 11
 ON_VECTOR_BUFS = 34
 
@@ -270,74 +270,72 @@ def tile_moe_rag_glu_sigmoid_kernel(tc, xT, w1, w3, w2, gate, offs, pos1, pos2, 
             sigmoids(e)
             for chunk in chunks(previous)[1:]:
                 gated(chunk)
-            quantise_hidden(previous)
+            if e != last:
+                quantise_hidden(previous)
         products("w3", last)
-        regroup_w2(first, 0, 128, SC)
+        regroup_w2(first, 128, N, SC)
+        regroup_w2(first, 0, 128, VE)
+        quantise_hidden(third)
         regroup_w2(second, 0, 128, VE)
-        regroup_w2(third, 0, 128, SC)
-        regroup_w2(last, 0, 128, SC)
         quantise_w2(first, 0, 128)
         multiply_w2(0, (first,))
         quantise_w2(second, 0, 128)
+        gated(chunks(last)[0])
+        regroup_w2(third, 0, 128, VE)
+        regroup_w2(last, 0, 128, SC)
+        quantise_hidden(last)
         quantise_w2(third, 0, 128)
         multiply_w2(0, (second, third))
-        regroup_w2(first, 128, 256, SC)
-        regroup_w2(first, 256, 384, SC)
-        gated(chunks(last)[0])
-        quantise_w2(last, 0, 128)
-        quantise_hidden(last)
-        multiply_w2(0, (last,))
         bring(0, (first,), SC)
-        regroup_w2(second, 128, 256, VE)
-        regroup_w2(third, 128, 256, VE)
-        regroup_w2(last, 128, 256, SC)
+        regroup_w2(second, 128, 256, SC)
+        quantise_w2(last, 0, 128)
+        multiply_w2(0, (last,))
+        quantise_w2(first, 128, N)
+        multiply_w2(1, (first,))
         bring(0, (second, third), SC)
         bring(0, (last,), SC)
-        quantise_w2(first, 128, 256)
-        multiply_w2(1, (first,))
+        regroup_w2(third, 128, 256, VE)
         quantise_w2(second, 128, 256)
+        regroup_w2(last, 128, 256, VE)
         quantise_w2(third, 128, 256)
         multiply_w2(1, (second, third))
+        fetch(0, 0)
         quantise_w2(last, 128, 256)
         multiply_w2(1, (last,))
-        fetch(0, 0)
+        multiply_w2(2, (first,))
         bring(1, (first,), SC)
         regroup_w2(second, 256, 384, SC)
         bring(1, (second, third), SC)
         bring(1, (last,), SC)
-        quantise_w2(first, 256, 384)
         fetch(0, 1)
         turn_and_add(0)
         regroup_w2(third, 256, 384, SC)
         regroup_w2(last, 256, 384, SC)
-        regroup_w2(first, 384, N, SC)
+        bring(2, (first,), SC)
+        regroup_w2(second, 384, N, SC)
         fetch(1, 0)
         quantise_w2(second, 256, 384)
         quantise_w2(third, 256, 384)
-        multiply_w2(2, (first,))
         multiply_w2(2, (second, third))
         quantise_w2(last, 256, 384)
         multiply_w2(2, (last,))
-        regroup_w2(second, 384, N, SC)
-        bring(2, (first,), SC)
+        multiply_w2(3, (first,))
+        regroup_w2(third, 384, N, SC)
         bring(2, (second, third), SC)
         bring(2, (last,), SC)
         fetch(1, 1)
-        quantise_w2(first, 384, N)
-        multiply_w2(3, (first,))
-        regroup_w2(third, 384, N, VE)
         regroup_w2(last, 384, N, VE)
         quantise_w2(second, 384, N)
         quantise_w2(third, 384, N)
         multiply_w2(3, (second, third))
         quantise_w2(last, 384, N)
         multiply_w2(3, (last,))
-        fetch(2, 0)
         turn_and_add(1)
-        turn_back(0)
+        fetch(2, 0)
         bring(3, (first,), SC)
         bring(3, (second, third), SC)
         bring(3, (last,), SC)
+        turn_back(0)
         turn_again(0)
         turn_back(1)
         turn_again(1)

@@ -195,7 +195,7 @@ def tile_moe_rag_glu_sigmoid_kernel(tc, xT, w1, w3, w2, gate, offs, pos1, pos2, 
         ys, y_sums = {}, {}
 
         def multiply_w2(t, experts):
-            a, b = STARTS[experts[0]], STARTS[experts[-1] + 1]
+            a, b = STARTS[min(experts)], STARTS[max(experts) + 1]
             py = bank([P, b - a], f"py{t}{experts[0]}")
             for e in experts:
                 codes, scales = w2_codes[t, e]
@@ -210,7 +210,7 @@ def tile_moe_rag_glu_sigmoid_kernel(tc, xT, w1, w3, w2, gate, offs, pos1, pos2, 
         def bring(t, experts, engine):
             if t not in ys:
                 ys[t] = made_by(nc.scalar, [P, S], F32, f"y{t}")
-            copy(engine, ys[t][:, STARTS[experts[0]]:STARTS[experts[-1] + 1]], y_sums[t, experts][:])
+            copy(engine, ys[t][:, STARTS[min(experts)]:STARTS[max(experts) + 1]], y_sums[t, experts][:])
 
         def outputs(t, experts, engine):
             multiply_w2(t, experts)
@@ -280,18 +280,18 @@ def tile_moe_rag_glu_sigmoid_kernel(tc, xT, w1, w3, w2, gate, offs, pos1, pos2, 
         quantise_w2(first, 0, 128)
         multiply_w2(0, (first,))
         quantise_w2(second, 0, 128)
-        gated(chunks(last)[0])
         regroup_w2(third, 0, 128, VE)
+        gated(chunks(last)[0])
         regroup_w2(last, 0, 128, SC)
-        quantise_hidden(last)
         quantise_w2(third, 0, 128)
         multiply_w2(0, (second, third))
+        quantise_hidden(last)
         bring(0, (first,), SC)
-        regroup_w2(second, 128, 256, SC)
         quantise_w2(last, 0, 128)
         multiply_w2(0, (last,))
         quantise_w2(first, 128, N)
         multiply_w2(1, (first,))
+        regroup_w2(second, 128, 256, SC)
         bring(0, (second, third), SC)
         bring(0, (last,), SC)
         regroup_w2(third, 128, 256, VE)
@@ -309,35 +309,35 @@ def tile_moe_rag_glu_sigmoid_kernel(tc, xT, w1, w3, w2, gate, offs, pos1, pos2, 
         bring(1, (last,), SC)
         fetch(0, 1)
         turn_and_add(0)
-        regroup_w2(third, 256, 384, SC)
-        regroup_w2(last, 256, 384, SC)
-        bring(2, (first,), SC)
-        regroup_w2(second, 384, N, SC)
-        fetch(1, 0)
+        regroup_w2(third, 256, 384, VE)
         quantise_w2(second, 256, 384)
+        regroup_w2(last, 256, 384, SC)
         quantise_w2(third, 256, 384)
         multiply_w2(2, (second, third))
+        regroup_w2(second, 384, N, SC)
+        regroup_w2(third, 384, N, SC)
+        bring(2, (first,), SC)
+        fetch(1, 0)
         quantise_w2(last, 256, 384)
         multiply_w2(2, (last,))
         multiply_w2(3, (first,))
-        regroup_w2(third, 384, N, SC)
         bring(2, (second, third), SC)
         bring(2, (last,), SC)
-        fetch(1, 1)
         regroup_w2(last, 384, N, VE)
         quantise_w2(second, 384, N)
+        fetch(1, 1)
         quantise_w2(third, 384, N)
         multiply_w2(3, (second, third))
         quantise_w2(last, 384, N)
         multiply_w2(3, (last,))
         turn_and_add(1)
-        fetch(2, 0)
+        turn_back(0)
         bring(3, (first,), SC)
         bring(3, (second, third), SC)
         bring(3, (last,), SC)
-        turn_back(0)
-        turn_again(0)
+        fetch(2, 0)
         turn_back(1)
+        turn_again(0)
         turn_again(1)
         store(0)
         store(1)

@@ -26,8 +26,8 @@ X_ON_SCALAR = 176
 IN_HALVES = ()
 W2_PIECES = ((0, 0, 512), (1, 0, 128), (2, 0, 128), (3, 0, 128), (1, 128, 256), (2, 128, 256), (3, 128, 256),
              (1, 256, 512), (2, 256, 512), (3, 256, 384), (3, 384, 512))
-W1_ON_SCALAR = (128, 32, 32, 40)
-W3_ON_SCALAR = (128, 128, 112, 80)
+W1_ON_SCALAR = (128, 32, 40, 48)
+W3_ON_SCALAR = (128, 128, 128, 88)
 ON_SCALAR_BUFS = 11
 ON_VECTOR_BUFS = 34
 
@@ -304,34 +304,32 @@ def tile_moe_rag_glu_sigmoid_kernel(tc, xT, w1, w3, w2, gate, offs, pos1, pos2, 
         multiply_w2(1, (last,))
         multiply_w2(2, (first,))
         bring(1, (first,), SC)
-        regroup_w2(second, 256, 384, SC)
+        regroup_w2(second, 256, N, SC)
         bring(1, (second, third), SC)
         bring(1, (last,), SC)
         fetch(0, 1)
         turn_and_add(0)
         regroup_w2(third, 256, 384, VE)
-        quantise_w2(second, 256, 384)
+        quantise_w2(second, 256, N)
         regroup_w2(last, 256, 384, SC)
         quantise_w2(third, 256, 384)
         multiply_w2(2, (second, third))
-        regroup_w2(second, 384, N, SC)
         regroup_w2(third, 384, N, SC)
         bring(2, (first,), SC)
         fetch(1, 0)
         quantise_w2(last, 256, 384)
         multiply_w2(2, (last,))
         multiply_w2(3, (first,))
+        turn_back(0)
         bring(2, (second, third), SC)
         bring(2, (last,), SC)
         regroup_w2(last, 384, N, VE)
-        quantise_w2(second, 384, N)
-        fetch(1, 1)
         quantise_w2(third, 384, N)
         multiply_w2(3, (second, third))
         quantise_w2(last, 384, N)
         multiply_w2(3, (last,))
+        fetch(1, 1)
         turn_and_add(1)
-        turn_back(0)
         bring(3, (first,), SC)
         bring(3, (second, third), SC)
         bring(3, (last,), SC)

@@ -18,39 +18,41 @@ MULT = mybir.AluOpType.mult
 ADD = mybir.AluOpType.add
 
 P = 128
+TILES = N // P
 FLOPS = 2 * S * (2 * K * H + H * N)
 
 ORDER = (1, 2, 3, 0)
-X_PIECES = ((0, 512),)
 X_ON_SCALAR = 176
-IN_HALVES = ()
-W2_PIECES = ((0, 0, 512), (1, 0, 128), (2, 0, 128), (3, 0, 128), (1, 128, 256), (2, 128, 256), (3, 128, 256),
-             (1, 256, 512), (2, 256, 512), (3, 256, 384), (3, 384, 512))
-W1_ON_SCALAR = (128, 32, 40, 48)
-W3_ON_SCALAR = (128, 128, 128, 88)
+W1_ON_SCALAR = 32
+LAST_W3_ON_SCALAR = 80
+ADDED_BY_TENSOR = 2
+CUT = 256
 ON_SCALAR_BUFS = 11
 ON_VECTOR_BUFS = 34
+PSUM_BANKS = 8
 
 
 def tile_moe_rag_glu_sigmoid_kernel(tc, xT, w1, w3, w2, gate, offs, pos1, pos2, out):
     nc = tc.nc
+    scalar, vector = nc.scalar, nc.vector
+    first, second, third, last = ORDER
     with ExitStack() as ctx:
         lists = ctx.enter_context(tc.tile_pool(name="lists", bufs=1))
         keep = ctx.enter_context(tc.tile_pool(name="keep", bufs=1))
         by_scalar = ctx.enter_context(tc.tile_pool(name="by_scalar", bufs=ON_SCALAR_BUFS))
         by_vector = ctx.enter_context(tc.tile_pool(name="by_vector", bufs=ON_VECTOR_BUFS))
-        psum = ctx.enter_context(tc.psum_pool(name="psum", bufs=8))
+        psum = ctx.enter_context(tc.psum_pool(name="psum", bufs=PSUM_BANKS))
 
         def made_by(engine, shape, dtype, name):
-            if engine is nc.scalar:
+            if engine is scalar:
                 return by_scalar.tile(shape, dtype, name=name, tag="s", align_bytes=64)
             return by_vector.tile(shape, dtype, name=name, tag="v", align_bytes=64)
 
         def copy(engine, dst, src):
-            if engine is nc.scalar:
-                nc.scalar.copy(out=dst, in_=src)
+            if engine is scalar:
+                scalar.copy(out=dst, in_=src)
             else:
-                nc.vector.tensor_copy(out=dst, in_=src)
+                vector.tensor_copy(out=dst, in_=src)
 
         def bank(shape, name):
             return psum.tile(shape, F32, name=name, tag="bank")
@@ -69,91 +71,69 @@ def tile_moe_rag_glu_sigmoid_kernel(tc, xT, w1, w3, w2, gate, offs, pos1, pos2, 
             nc.sync.dma_start(out=raw[:], in_=src.rearrange("(p j) c -> p j c", j=4))
             return raw
 
-        first, second, third, last = ORDER
-        x_raw = [load_rows(xT[:, a:b], f"x_raw{a}") for a, b in X_PIECES]
+        x_raw = load_rows(xT[:, 0:T], "x_raw")
         gate_cols = keep.tile([P, 2, 8], F32, name="gate_cols")
-        nc.scalar.dma_start(out=gate_cols[:, :, 0:4], in_=gate[:, 0, :].rearrange("c (p j) -> p c j", j=4))
+        scalar.dma_start(out=gate_cols[:, :, 0:4], in_=gate[:, 0, :].rearrange("c (p j) -> p c j", j=4))
         nc.sync.dma_start(offs_sb[:], offs)
         w_raw, w2_raw = {}, {}
         for e in ORDER:
-            for nm, w in (("w1", w1), ("w3", w3)):
-                width = H // 2 if (nm, e) in IN_HALVES else H
-                w_raw[nm, e] = [load_rows(w[e, :, a:a + width], f"{nm}_raw{e}_{a}") for a in range(0, H, width)]
+            w_raw["w1", e] = load_rows(w1[e, :, 0:H], f"w1_raw{e}")
+            w_raw["w3", e] = load_rows(w3[e, :, 0:H], f"w3_raw{e}")
             if e == second:
                 nc.sync.dma_start(pos1_sb[:], pos1)
                 nc.sync.dma_start(pos2_sb[:], pos2)
-        for i, a, b in W2_PIECES:
-            e = ORDER[i]
-            raw = load_rows(w2[e, :, a:b], f"w2_raw{e}_{a}")
-            for col in range(a, b, P):
-                w2_raw[e, col] = (raw, a)
+        first_w2 = load_rows(w2[first, :, 0:N], "w2_raw_first")
+        for t in range(TILES):
+            for e in (second, third, last):
+                w2_raw[e, t] = load_rows(w2[e, :, t * P:(t + 1) * P], f"w2_raw{e}_{t}")
 
-        warm = made_by(nc.scalar, [P, 1], F32, "warm")
-        nc.scalar.activation(out=warm[:], in_=identity[:, 0:1], func=SIGMOID)
-
-        gate_rows = {}
-
-        def spread_gate(c, engine):
-            spread = bank([P, 4, P], f"spread{c}")
-            for j in range(4):
-                nc.tensor.transpose(spread[:, j, :], gate_cols[:, c, j:j + 1].to_broadcast([P, P]), identity[:])
-            gate_rows[c] = made_by(engine, [P, T], F32, f"gate_rows{c}")
-            copy(engine, gate_rows[c][:].rearrange("p (i j) -> p i j", j=4), spread[:].rearrange("p j i -> p i j"))
-
+        warm = made_by(scalar, [P, 1], F32, "warm")
+        scalar.activation(out=warm[:], in_=identity[:, 0:1], func=SIGMOID)
 
         def interleave(engine, grouped, raw):
             copy(engine, grouped.rearrange("p (c i) j -> p c j i", i=4), raw.rearrange("p j (c i) -> p c j i", i=4))
 
-        x_words = made_by(nc.vector, [P, T], U32, "x_words")
-        x_grouped = []
-        for raw, (a, b) in zip(x_raw, X_PIECES):
-            share = X_ON_SCALAR if b == T else 0
-            x_grouped.append(made_by(nc.scalar if share else nc.vector, [P, b - a, 4], BF16, f"x_grouped{a}"))
-            if share:
-                interleave(nc.scalar, x_grouped[-1][:, 0:share, :], raw[:, :, 0:share])
-            interleave(nc.vector, x_grouped[-1][:, share:b - a, :], raw[:, :, share:b - a])
-            if b == T:
-                spread_gate(0, nc.scalar)
-                spread_gate(1, nc.scalar)
-            nc.vector.quantize_mx(out=x_words[:, a:b].bitcast(FP8X4), scales=x_scales[:, a:b],
-                                  in_=x_grouped[-1][:].rearrange("p c j -> p (c j)"))
-
-        slot_words, slot_scales = {}, {}
-
-        def gather_tokens(e):
-            a, b = STARTS[e], STARTS[e + 1]
-            idx = offs_sb[:, a // 16:b // 16]
-            slot_words[e] = made_by(nc.vector, [P, b - a], U32, f"slot_words{e}")
-            nc.vector.tensor_copy(out=slot_words[e][:], in_=x_words[:].indirect(idx))
-            slot_scales[e] = made_by(nc.vector, [P, b - a], U8, f"slot_scales{e}")
-            nc.vector.tensor_copy(out=slot_scales[e][:], in_=x_scales[:].indirect(idx))
-
-        grouped = {}
-
-        def regroup(nm, e, share):
-            grouped[nm, e] = made_by(nc.scalar, [P, 4, P, 4], BF16, f"g{nm}{e}")
-            width = P // len(w_raw[nm, e])
-            for k, raw in enumerate(w_raw[nm, e]):
-                cut = min(max(share - k * width, 0), width)
-                piece = grouped[nm, e][:, :, k * width:(k + 1) * width, :]
-                if cut > 0:
-                    nc.scalar.copy(out=piece.rearrange("p t m j -> p m j t")[:, 0:cut],
-                                   in_=raw[:].rearrange("p j (m t) -> p m j t", t=4)[:, 0:cut])
-                if cut < width:
-                    nc.vector.tensor_copy(out=piece.rearrange("p (u v) m j -> p u m j v", v=2)[:, :, cut:width],
-                                          in_=raw[:].rearrange("p j (m u v) -> p u m j v", u=2, v=2)[:, :, cut:width])
-
         def quantise(source, name):
             width = source.shape[1] // 4
-            codes = made_by(nc.vector, [P, width], U32, f"q{name}")
+            codes = made_by(vector, [P, width], U32, f"q{name}")
             scales = keep.tile([P, width], U8, name=f"scales{name}", align_bytes=64)
-            nc.vector.quantize_mx(out=codes[:].bitcast(FP8X4), scales=scales[:], in_=source)
+            vector.quantize_mx(out=codes[:].bitcast(FP8X4), scales=scales[:], in_=source)
             return codes, scales
+
+        x_words = made_by(vector, [P, T], U32, "x_words")
+        x_grouped = made_by(scalar, [P, T, 4], BF16, "x_grouped")
+        interleave(scalar, x_grouped[:, 0:X_ON_SCALAR, :], x_raw[:, :, 0:X_ON_SCALAR])
+        interleave(vector, x_grouped[:, X_ON_SCALAR:T, :], x_raw[:, :, X_ON_SCALAR:T])
+        gate_rows = []
+        for c in range(2):
+            spread = bank([P, 4, P], f"spread{c}")
+            for j in range(4):
+                nc.tensor.transpose(spread[:, j, :], gate_cols[:, c, j:j + 1].to_broadcast([P, P]), identity[:])
+            gate_rows.append(made_by(scalar, [P, T], F32, f"gate_rows{c}"))
+            scalar.copy(out=gate_rows[c][:].rearrange("p (i j) -> p i j", j=4), in_=spread[:].rearrange("p j i -> p i j"))
+        vector.quantize_mx(out=x_words[:, 0:T].bitcast(FP8X4), scales=x_scales[:, 0:T], in_=x_grouped[:].rearrange("p c j -> p (c j)"))
+
+        slot_words, slot_scales, grouped, sums, sigs, hidden, h_codes = {}, {}, {}, {}, {}, {}, {}
 
         def chunks(e):
             return range(STARTS[e] // P, STARTS[e + 1] // P)
 
-        sums, sigs, hidden, h_codes = {}, {}, {}, {}
+        def gather_tokens(e):
+            a, b = STARTS[e], STARTS[e + 1]
+            idx = offs_sb[:, a // 16:b // 16]
+            slot_words[e] = made_by(vector, [P, b - a], U32, f"slot_words{e}")
+            vector.tensor_copy(out=slot_words[e][:], in_=x_words[:].indirect(idx))
+            slot_scales[e] = made_by(vector, [P, b - a], U8, f"slot_scales{e}")
+            vector.tensor_copy(out=slot_scales[e][:], in_=x_scales[:].indirect(idx))
+
+        def regroup(nm, e, on_scalar):
+            grouped[nm, e] = made_by(scalar, [P, 4, P, 4], BF16, f"g{nm}{e}")
+            raw = w_raw[nm, e]
+            scalar.copy(out=grouped[nm, e][:].rearrange("p t m j -> p m j t")[:, 0:on_scalar],
+                        in_=raw[:].rearrange("p j (m t) -> p m j t", t=4)[:, 0:on_scalar])
+            if on_scalar < P:
+                vector.tensor_copy(out=grouped[nm, e][:].rearrange("p (u v) m j -> p u m j v", v=2)[:, :, on_scalar:P],
+                                   in_=raw[:].rearrange("p j (m u v) -> p u m j v", u=2, v=2)[:, :, on_scalar:P])
 
         def products(nm, e):
             codes, scales = quantise(grouped[nm, e][:].rearrange("p t m j -> p (t m j)"), f"{nm}{e}")
@@ -169,59 +149,83 @@ def tile_moe_rag_glu_sigmoid_kernel(tc, xT, w1, w3, w2, gate, offs, pos1, pos2, 
 
         def sigmoids(e):
             for chunk in chunks(e):
-                sigs[chunk] = made_by(nc.scalar, [P, P, 4], F32, f"sig{chunk}")
-                nc.scalar.activation(out=sigs[chunk][:], in_=sums["w1", chunk][:].rearrange("p t n -> p n t"), func=SIGMOID)
+                sigs[chunk] = made_by(scalar, [P, P, 4], F32, f"sig{chunk}")
+                scalar.activation(out=sigs[chunk][:], in_=sums["w1", chunk][:].rearrange("p t n -> p n t"), func=SIGMOID)
 
         def gated(chunk):
-            hidden[chunk] = made_by(nc.vector, [P, P, 4], BF16, f"hidden{chunk}")
-            nc.vector.tensor_tensor(out=hidden[chunk][:], in0=sums["w3", chunk][:].rearrange("p t n -> p n t"), in1=sigs[chunk][:], op=MULT)
+            hidden[chunk] = made_by(vector, [P, P, 4], BF16, f"hidden{chunk}")
+            vector.tensor_tensor(out=hidden[chunk][:], in0=sums["w3", chunk][:].rearrange("p t n -> p n t"), in1=sigs[chunk][:], op=MULT)
 
         def quantise_hidden(e):
             for chunk in chunks(e):
                 h_codes[chunk] = quantise(hidden[chunk][:].rearrange("p n t -> p (n t)"), f"h{chunk}")
 
-        w2_grouped, w2_codes = {}, {}
+        gather_tokens(first)
+        gather_tokens(second)
+        regroup("w1", first, P)
+        products("w1", first)
+        gather_tokens(third)
+        gather_tokens(last)
+        regroup("w3", first, P)
+        sigmoids(first)
+        for previous, e in zip(ORDER, ORDER[1:]):
+            products("w3", previous)
+            regroup("w1", e, W1_ON_SCALAR)
+            gated(chunks(previous)[0])
+            products("w1", e)
+            regroup("w3", e, P if e != last else LAST_W3_ON_SCALAR)
+            sigmoids(e)
+            for chunk in chunks(previous)[1:]:
+                gated(chunk)
+            if e != last:
+                quantise_hidden(previous)
+        products("w3", last)
 
-        def regroup_w2(e, a, b, engine):
-            w2_grouped[e, a] = made_by(engine, [P, b - a, 4], BF16, f"gw2{e}_{a}")
-            raw, start = w2_raw[e, a]
-            interleave(engine, w2_grouped[e, a][:], raw[:, :, a - start:b - start])
+        w2_grouped, w2_codes, ys, y_sums, parts, turned, by_token = {}, {}, {}, {}, {}, {}, {}
+        banks = ((first,), (second, third), (last,))
 
-        def quantise_w2(e, a, b):
-            codes, scales = quantise(w2_grouped[e, a][:].rearrange("p c j -> p (c j)"), f"w2{e}_{a}")
-            for col in range(a, b, P):
-                w2_codes[col // P, e] = (codes[:, col - a:col - a + P], scales[:, col - a:col - a + P])
+        def regroup_w2(engine, e, t, raw):
+            w2_grouped[e, t] = made_by(engine, [P, raw.shape[2], 4], BF16, f"gw2{e}_{t}")
+            interleave(engine, w2_grouped[e, t][:], raw)
 
-        ys, y_sums = {}, {}
+        def quantise_w2(e, t):
+            codes, scales = quantise(w2_grouped[e, t][:].rearrange("p c j -> p (c j)"), f"w2{e}_{t}")
+            for k in range(codes.shape[1] // P):
+                w2_codes[e, t + k] = (codes[:, k * P:(k + 1) * P], scales[:, k * P:(k + 1) * P])
 
         def multiply_w2(t, experts):
-            a, b = STARTS[min(experts)], STARTS[max(experts) + 1]
-            py = bank([P, b - a], f"py{t}{experts[0]}")
+            a, b = STARTS[experts[0]], STARTS[experts[-1] + 1]
+            y_sums[t, experts] = bank([P, b - a], f"py{t}{experts[0]}")
             for e in experts:
-                codes, scales = w2_codes[t, e]
+                codes, scales = w2_codes[e, t]
                 for chunk in chunks(e):
                     place = chunk * P - a
-                    nc.tensor.matmul_mx(out=py[:, place:place + P],
+                    nc.tensor.matmul_mx(out=y_sums[t, experts][:, place:place + P],
                                         lhsT=codes.bitcast(FP8X4), lhsT_scale=scales,
                                         rhs=h_codes[chunk][0][:].bitcast(FP8X4), rhs_scale=h_codes[chunk][1][:],
                                         start=True, stop=True)
-            y_sums[t, experts] = py
 
-        def bring(t, experts, engine):
-            if t not in ys:
-                ys[t] = made_by(nc.scalar, [P, S], F32, f"y{t}")
-            copy(engine, ys[t][:, STARTS[min(experts)]:STARTS[max(experts) + 1]], y_sums[t, experts][:])
+        def regroup_tile(engine, t):
+            for e in (second, third, last):
+                if (e == last) == (engine is vector):
+                    regroup_w2(engine, e, t, w2_raw[e, t][:])
 
-        def outputs(t, experts, engine):
-            multiply_w2(t, experts)
-            bring(t, experts, engine)
+        def multiply_tile(t):
+            multiply_w2(t, banks[0])
+            for experts in banks[1:]:
+                for e in experts:
+                    quantise_w2(e, t)
+                multiply_w2(t, experts)
 
-        parts, turned = {}, {}
+        def bring(t):
+            ys[t] = made_by(scalar, [P, S], F32, f"y{t}")
+            for experts in banks:
+                scalar.copy(out=ys[t][:, STARTS[experts[0]]:STARTS[experts[-1] + 1]], in_=y_sums[t, experts][:])
 
         def fetch(t, c, a=0, b=T):
-            parts[t, c, a] = made_by(nc.vector, [P, b - a], F32, f"part{t}{c}_{a}")
+            parts[t, c, a] = made_by(vector, [P, b - a], F32, f"part{t}{c}_{a}")
             idx = (pos1_sb, pos2_sb)[c][:, a // 16:b // 16]
-            nc.vector.tensor_tensor(out=parts[t, c, a][:], in0=ys[t][:].indirect(idx), in1=gate_rows[c][:, a:b], op=MULT)
+            vector.tensor_tensor(out=parts[t, c, a][:], in0=ys[t][:].indirect(idx), in1=gate_rows[c][:, a:b], op=MULT)
 
         def turn_and_add(t):
             turned[t] = bank([P, 4, P], f"turned{t}")
@@ -231,119 +235,67 @@ def tile_moe_rag_glu_sigmoid_kernel(tc, xT, w1, w3, w2, gate, offs, pos1, pos2, 
                     nc.tensor.matmul(out=turned[t][:, b, :], lhsT=parts[t, c, 0][:, cols], rhs=identity[:],
                                      start=(c == 0), stop=(c == 1), is_transpose=True)
 
-        def turn_back(t):
-            by_token = made_by(nc.scalar, [P, 4, P], F32, f"by_token{t}")
-            nc.scalar.copy(out=by_token[:], in_=turned[t][:])
-            parts[t] = by_token
+        def leave_psum(t):
+            by_token[t] = made_by(scalar, [P, 4, P], F32, f"by_token{t}")
+            scalar.copy(out=by_token[t][:], in_=turned[t][:])
 
-        def turn_again(t):
+        def turn_back(t):
             turned[t] = bank([P, 4, P], f"summed{t}")
             for b in range(4):
-                nc.tensor.transpose(turned[t][:, b, :], parts[t][:, b, :], identity[:])
+                nc.tensor.transpose(turned[t][:, b, :], by_token[t][:, b, :], identity[:])
 
-        def store(t):
-            total = made_by(nc.scalar, [P, T], F32, f"total{t}")
-            nc.scalar.copy(out=total[:], in_=turned[t][:].rearrange("p b i -> p (b i)"))
-            nc.scalar.dma_start(out=out[t * P:(t + 1) * P, :], in_=total[:])
+        def store_turned(t):
+            total = made_by(scalar, [P, T], F32, f"total{t}")
+            scalar.copy(out=total[:], in_=turned[t][:].rearrange("p b i -> p (b i)"))
+            scalar.dma_start(out=out[t * P:(t + 1) * P, :], in_=total[:])
 
-        def finish(t, a=0, b=T):
-            total = made_by(nc.vector, [P, b - a], F32, f"total{t}_{a}")
-            nc.vector.tensor_tensor(out=total[:], in0=parts[t, 0, a][:], in1=parts[t, 1, a][:], op=ADD)
+        def add_and_store(t, a=0, b=T):
+            total = made_by(vector, [P, b - a], F32, f"total{t}_{a}")
+            vector.tensor_tensor(out=total[:], in0=parts[t, 0, a][:], in1=parts[t, 1, a][:], op=ADD)
             nc.sync.dma_start(out=out[t * P:(t + 1) * P, a:b], in_=total[:])
 
-        SC, VE = nc.scalar, nc.vector
-        gather_tokens(first)
-        gather_tokens(second)
-        regroup("w1", first, W1_ON_SCALAR[0])
-        products("w1", first)
-        gather_tokens(third)
-        gather_tokens(last)
-        regroup("w3", first, W3_ON_SCALAR[0])
-        sigmoids(first)
-        for i in range(1, E):
-            previous, e = ORDER[i - 1], ORDER[i]
-            products("w3", previous)
-            regroup("w1", e, W1_ON_SCALAR[i])
-            gated(chunks(previous)[0])
-            products("w1", e)
-            regroup("w3", e, W3_ON_SCALAR[i])
-            sigmoids(e)
-            for chunk in chunks(previous)[1:]:
-                gated(chunk)
-            if e != last:
-                quantise_hidden(previous)
-        products("w3", last)
-        regroup_w2(first, 128, N, SC)
-        regroup_w2(first, 0, 128, VE)
+        regroup_w2(scalar, first, 1, first_w2[:, :, P:N])
+        regroup_w2(vector, first, 0, first_w2[:, :, 0:P])
         quantise_hidden(third)
-        regroup_w2(second, 0, 128, VE)
-        quantise_w2(first, 0, 128)
-        multiply_w2(0, (first,))
-        quantise_w2(second, 0, 128)
-        regroup_w2(third, 0, 128, VE)
+        regroup_w2(vector, second, 0, w2_raw[second, 0][:])
+        quantise_w2(first, 0)
+        multiply_w2(0, banks[0])
+        quantise_w2(second, 0)
+        regroup_w2(vector, third, 0, w2_raw[third, 0][:])
         gated(chunks(last)[0])
-        regroup_w2(last, 0, 128, SC)
-        quantise_w2(third, 0, 128)
-        multiply_w2(0, (second, third))
+        regroup_w2(scalar, last, 0, w2_raw[last, 0][:])
+        quantise_w2(third, 0)
+        multiply_w2(0, banks[1])
         quantise_hidden(last)
-        bring(0, (first,), SC)
-        quantise_w2(last, 0, 128)
-        multiply_w2(0, (last,))
-        quantise_w2(first, 128, N)
-        multiply_w2(1, (first,))
-        regroup_w2(second, 128, 256, SC)
-        bring(0, (second, third), SC)
-        bring(0, (last,), SC)
-        regroup_w2(third, 128, 256, VE)
-        quantise_w2(second, 128, 256)
-        regroup_w2(last, 128, 256, VE)
-        quantise_w2(third, 128, 256)
-        multiply_w2(1, (second, third))
-        fetch(0, 0)
-        quantise_w2(last, 128, 256)
-        multiply_w2(1, (last,))
-        multiply_w2(2, (first,))
-        bring(1, (first,), SC)
-        regroup_w2(second, 256, N, SC)
-        bring(1, (second, third), SC)
-        bring(1, (last,), SC)
-        fetch(0, 1)
-        turn_and_add(0)
-        regroup_w2(third, 256, 384, VE)
-        quantise_w2(second, 256, N)
-        regroup_w2(last, 256, 384, SC)
-        quantise_w2(third, 256, 384)
-        multiply_w2(2, (second, third))
-        regroup_w2(third, 384, N, SC)
-        bring(2, (first,), SC)
-        fetch(1, 0)
-        quantise_w2(last, 256, 384)
-        multiply_w2(2, (last,))
-        multiply_w2(3, (first,))
-        turn_back(0)
-        bring(2, (second, third), SC)
-        bring(2, (last,), SC)
-        regroup_w2(last, 384, N, VE)
-        quantise_w2(third, 384, N)
-        multiply_w2(3, (second, third))
-        quantise_w2(last, 384, N)
-        multiply_w2(3, (last,))
-        fetch(1, 1)
-        turn_and_add(1)
-        bring(3, (first,), SC)
-        bring(3, (second, third), SC)
-        bring(3, (last,), SC)
-        fetch(2, 0)
-        turn_back(1)
-        turn_again(0)
-        turn_again(1)
-        store(0)
-        store(1)
-        fetch(2, 1)
-        fetch(3, 0, 0, 256)
-        finish(2)
-        fetch(3, 1, 0, 256)
-        fetch(3, 0, 256, T)
-        fetch(3, 1, 256, T)
-        finish(3, 0, 256)
-        finish(3, 256, T)
+        quantise_w2(last, 0)
+        multiply_w2(0, banks[2])
+        quantise_w2(first, 1)
+
+        for t in range(TILES):
+            following = t + 1 < TILES
+            if following:
+                regroup_tile(scalar, t + 1)
+            bring(t)
+            if 0 <= t - 2 < ADDED_BY_TENSOR:
+                leave_psum(t - 2)
+            if following:
+                regroup_tile(vector, t + 1)
+                multiply_tile(t + 1)
+            if 0 <= t - 1 < ADDED_BY_TENSOR:
+                turn_and_add(t - 1)
+            if following:
+                fetch(t, 0)
+                fetch(t, 1)
+        for t in range(ADDED_BY_TENSOR):
+            turn_back(t)
+        for t in range(ADDED_BY_TENSOR):
+            store_turned(t)
+
+        end = TILES - 1
+        fetch(end, 0, 0, CUT)
+        add_and_store(end - 1)
+        fetch(end, 1, 0, CUT)
+        fetch(end, 0, CUT, T)
+        fetch(end, 1, CUT, T)
+        add_and_store(end, 0, CUT)
+        add_and_store(end, CUT, T)

@@ -25,7 +25,7 @@ ORDER = (1, 2, 3, 0)
 X_ON_SCALAR = 176
 W1_ON_SCALAR = 32
 LAST_W3_ON_SCALAR = 80
-ADDED_BY_TENSOR = 2
+ADDED_BY_TENSOR = 1
 CUT = 256
 ON_SCALAR_BUFS = 11
 ON_VECTOR_BUFS = 34
@@ -285,6 +285,8 @@ def tile_moe_rag_glu_sigmoid_kernel(tc, xT, w1, w3, w2, gate, offs, pos1, pos2, 
                 turn_and_add(t - 1)
             if following:
                 fetch(t, 0)
+                if ADDED_BY_TENSOR <= t - 1:
+                    add_and_store(t - 1)
                 fetch(t, 1)
         for t in range(ADDED_BY_TENSOR):
             turn_back(t)

from contextlib import ExitStack

import concourse.mybir as mybir
from concourse.masks import make_identity

K, T, E, H, N = 512, 512, 4, 512, 512
STARTS = (0, 128, 512, 768, 1024)
S = 1024

F32 = mybir.dt.float32
BF16 = mybir.dt.bfloat16
U32 = mybir.dt.uint32
U16 = mybir.dt.uint16
U8 = mybir.dt.uint8
FP8X4 = mybir.dt.float8_e4m3fn_x4
SIGMOID = mybir.ActivationFunctionType.Sigmoid
MULT = mybir.AluOpType.mult
ADD = mybir.AluOpType.add

P = 128
TILES = N // P
FLOPS = 2 * S * (2 * K * H + H * N)

ORDER = (1, 2, 3, 0)
X_ON_SCALAR = 176
W1_ON_SCALAR = 32
LAST_W3_ON_SCALAR = 80
ADDED_BY_TENSOR = 1
CUT = 256
ON_SCALAR_BUFS = 11
ON_VECTOR_BUFS = 34
PSUM_BANKS = 8


def tile_moe_rag_glu_sigmoid_kernel(tc, xT, w1, w3, w2, gate, offs, pos1, pos2, out):
    nc = tc.nc
    scalar, vector = nc.scalar, nc.vector
    first, second, third, last = ORDER
    with ExitStack() as ctx:
        lists = ctx.enter_context(tc.tile_pool(name="lists", bufs=1))
        keep = ctx.enter_context(tc.tile_pool(name="keep", bufs=1))
        by_scalar = ctx.enter_context(tc.tile_pool(name="by_scalar", bufs=ON_SCALAR_BUFS))
        by_vector = ctx.enter_context(tc.tile_pool(name="by_vector", bufs=ON_VECTOR_BUFS))
        psum = ctx.enter_context(tc.psum_pool(name="psum", bufs=PSUM_BANKS))

        def made_by(engine, shape, dtype, name):
            if engine is scalar:
                return by_scalar.tile(shape, dtype, name=name, tag="s", align_bytes=64)
            return by_vector.tile(shape, dtype, name=name, tag="v", align_bytes=64)

        def copy(engine, dst, src):
            if engine is scalar:
                scalar.copy(out=dst, in_=src)
            else:
                vector.tensor_copy(out=dst, in_=src)

        def bank(shape, name):
            return psum.tile(shape, F32, name=name, tag="bank")

        offs_sb = lists.tile([P, S // 16], U16, name="offs_sb")
        pos1_sb = lists.tile([P, T // 16], U16, name="pos1_sb")
        pos2_sb = lists.tile([P, T // 16], U16, name="pos2_sb")

        x_scales = keep.tile([P, T], U8, name="x_scales", align_bytes=64)
        nc.gpsimd.memset(x_scales[:], 0)
        identity = keep.tile([P, P], F32, name="identity")
        make_identity(nc, identity[:])

        def load_rows(src, name):
            raw = keep.tile([P, 4, src.shape[1]], F32, name=name, align_bytes=256)
            nc.sync.dma_start(out=raw[:], in_=src.rearrange("(p j) c -> p j c", j=4))
            return raw

        x_raw = load_rows(xT[:, 0:T], "x_raw")
        gate_cols = keep.tile([P, 2, 8], F32, name="gate_cols")
        scalar.dma_start(out=gate_cols[:, :, 0:4], in_=gate[:, 0, :].rearrange("c (p j) -> p c j", j=4))
        nc.sync.dma_start(offs_sb[:], offs)
        w_raw, w2_raw = {}, {}
        for e in ORDER:
            w_raw["w1", e] = load_rows(w1[e, :, 0:H], f"w1_raw{e}")
            w_raw["w3", e] = load_rows(w3[e, :, 0:H], f"w3_raw{e}")
            if e == second:
                nc.sync.dma_start(pos1_sb[:], pos1)
                nc.sync.dma_start(pos2_sb[:], pos2)
        first_w2 = load_rows(w2[first, :, 0:N], "w2_raw_first")
        for t in range(TILES):
            for e in (second, third, last):
                w2_raw[e, t] = load_rows(w2[e, :, t * P:(t + 1) * P], f"w2_raw{e}_{t}")

        warm = made_by(scalar, [P, 1], F32, "warm")
        scalar.activation(out=warm[:], in_=identity[:, 0:1], func=SIGMOID)

        def interleave(engine, grouped, raw):
            copy(engine, grouped.rearrange("p (c i) j -> p c j i", i=4), raw.rearrange("p j (c i) -> p c j i", i=4))

        def quantise(source, name):
            width = source.shape[1] // 4
            codes = made_by(vector, [P, width], U32, f"q{name}")
            scales = keep.tile([P, width], U8, name=f"scales{name}", align_bytes=64)
            vector.quantize_mx(out=codes[:].bitcast(FP8X4), scales=scales[:], in_=source)
            return codes, scales

        x_words = made_by(vector, [P, T], U32, "x_words")
        x_grouped = made_by(scalar, [P, T, 4], BF16, "x_grouped")
        interleave(scalar, x_grouped[:, 0:X_ON_SCALAR, :], x_raw[:, :, 0:X_ON_SCALAR])
        interleave(vector, x_grouped[:, X_ON_SCALAR:T, :], x_raw[:, :, X_ON_SCALAR:T])
        gate_rows = []
        for c in range(2):
            spread = bank([P, 4, P], f"spread{c}")
            for j in range(4):
                nc.tensor.transpose(spread[:, j, :], gate_cols[:, c, j:j + 1].to_broadcast([P, P]), identity[:])
            gate_rows.append(made_by(scalar, [P, T], F32, f"gate_rows{c}"))
            scalar.copy(out=gate_rows[c][:].rearrange("p (i j) -> p i j", j=4), in_=spread[:].rearrange("p j i -> p i j"))
        vector.quantize_mx(out=x_words[:, 0:T].bitcast(FP8X4), scales=x_scales[:, 0:T], in_=x_grouped[:].rearrange("p c j -> p (c j)"))

        slot_words, slot_scales, grouped, sums, sigs, hidden, h_codes = {}, {}, {}, {}, {}, {}, {}

        def chunks(e):
            return range(STARTS[e] // P, STARTS[e + 1] // P)

        def gather_tokens(e):
            a, b = STARTS[e], STARTS[e + 1]
            idx = offs_sb[:, a // 16:b // 16]
            slot_words[e] = made_by(vector, [P, b - a], U32, f"slot_words{e}")
            vector.tensor_copy(out=slot_words[e][:], in_=x_words[:].indirect(idx))
            slot_scales[e] = made_by(vector, [P, b - a], U8, f"slot_scales{e}")
            vector.tensor_copy(out=slot_scales[e][:], in_=x_scales[:].indirect(idx))

        def regroup(nm, e, on_scalar):
            grouped[nm, e] = made_by(scalar, [P, 4, P, 4], BF16, f"g{nm}{e}")
            raw = w_raw[nm, e]
            scalar.copy(out=grouped[nm, e][:].rearrange("p t m j -> p m j t")[:, 0:on_scalar],
                        in_=raw[:].rearrange("p j (m t) -> p m j t", t=4)[:, 0:on_scalar])
            if on_scalar < P:
                vector.tensor_copy(out=grouped[nm, e][:].rearrange("p (u v) m j -> p u m j v", v=2)[:, :, on_scalar:P],
                                   in_=raw[:].rearrange("p j (m u v) -> p u m j v", u=2, v=2)[:, :, on_scalar:P])

        def products(nm, e):
            codes, scales = quantise(grouped[nm, e][:].rearrange("p t m j -> p (t m j)"), f"{nm}{e}")
            for chunk in chunks(e):
                slots = slice(chunk * P - STARTS[e], (chunk + 1) * P - STARTS[e])
                sums[nm, chunk] = bank([P, 4, P], f"p{nm}{chunk}")
                for t in range(4):
                    cols = slice(t * P, (t + 1) * P)
                    nc.tensor.matmul_mx(out=sums[nm, chunk][:, t, :],
                                        lhsT=codes[:, cols].bitcast(FP8X4), lhsT_scale=scales[:, cols],
                                        rhs=slot_words[e][:, slots].bitcast(FP8X4), rhs_scale=slot_scales[e][:, slots],
                                        start=True, stop=True)

        def sigmoids(e):
            for chunk in chunks(e):
                sigs[chunk] = made_by(scalar, [P, P, 4], F32, f"sig{chunk}")
                scalar.activation(out=sigs[chunk][:], in_=sums["w1", chunk][:].rearrange("p t n -> p n t"), func=SIGMOID)

        def gated(chunk):
            hidden[chunk] = made_by(vector, [P, P, 4], BF16, f"hidden{chunk}")
            vector.tensor_tensor(out=hidden[chunk][:], in0=sums["w3", chunk][:].rearrange("p t n -> p n t"), in1=sigs[chunk][:], op=MULT)

        def quantise_hidden(e):
            for chunk in chunks(e):
                h_codes[chunk] = quantise(hidden[chunk][:].rearrange("p n t -> p (n t)"), f"h{chunk}")

        gather_tokens(first)
        gather_tokens(second)
        regroup("w1", first, P)
        products("w1", first)
        gather_tokens(third)
        gather_tokens(last)
        regroup("w3", first, P)
        sigmoids(first)
        for previous, e in zip(ORDER, ORDER[1:]):
            products("w3", previous)
            regroup("w1", e, W1_ON_SCALAR)
            gated(chunks(previous)[0])
            products("w1", e)
            regroup("w3", e, P if e != last else LAST_W3_ON_SCALAR)
            sigmoids(e)
            for chunk in chunks(previous)[1:]:
                gated(chunk)
            if e != last:
                quantise_hidden(previous)
        products("w3", last)

        w2_grouped, w2_codes, ys, y_sums, parts, turned, by_token = {}, {}, {}, {}, {}, {}, {}
        banks = ((first,), (second, third), (last,))

        def regroup_w2(engine, e, t, raw):
            w2_grouped[e, t] = made_by(engine, [P, raw.shape[2], 4], BF16, f"gw2{e}_{t}")
            interleave(engine, w2_grouped[e, t][:], raw)

        def quantise_w2(e, t):
            codes, scales = quantise(w2_grouped[e, t][:].rearrange("p c j -> p (c j)"), f"w2{e}_{t}")
            for k in range(codes.shape[1] // P):
                w2_codes[e, t + k] = (codes[:, k * P:(k + 1) * P], scales[:, k * P:(k + 1) * P])

        def multiply_w2(t, experts):
            a, b = STARTS[experts[0]], STARTS[experts[-1] + 1]
            y_sums[t, experts] = bank([P, b - a], f"py{t}{experts[0]}")
            for e in experts:
                codes, scales = w2_codes[e, t]
                for chunk in chunks(e):
                    place = chunk * P - a
                    nc.tensor.matmul_mx(out=y_sums[t, experts][:, place:place + P],
                                        lhsT=codes.bitcast(FP8X4), lhsT_scale=scales,
                                        rhs=h_codes[chunk][0][:].bitcast(FP8X4), rhs_scale=h_codes[chunk][1][:],
                                        start=True, stop=True)

        def regroup_tile(engine, t):
            for e in (second, third, last):
                if (e == last) == (engine is vector):
                    regroup_w2(engine, e, t, w2_raw[e, t][:])

        def multiply_tile(t):
            multiply_w2(t, banks[0])
            for experts in banks[1:]:
                for e in experts:
                    quantise_w2(e, t)
                multiply_w2(t, experts)

        def bring(t):
            ys[t] = made_by(scalar, [P, S], F32, f"y{t}")
            for experts in banks:
                scalar.copy(out=ys[t][:, STARTS[experts[0]]:STARTS[experts[-1] + 1]], in_=y_sums[t, experts][:])

        def fetch(t, c, a=0, b=T):
            parts[t, c, a] = made_by(vector, [P, b - a], F32, f"part{t}{c}_{a}")
            idx = (pos1_sb, pos2_sb)[c][:, a // 16:b // 16]
            vector.tensor_tensor(out=parts[t, c, a][:], in0=ys[t][:].indirect(idx), in1=gate_rows[c][:, a:b], op=MULT)

        def turn_and_add(t):
            turned[t] = bank([P, 4, P], f"turned{t}")
            for b in range(4):
                cols = slice(b * P, (b + 1) * P)
                for c in range(2):
                    nc.tensor.matmul(out=turned[t][:, b, :], lhsT=parts[t, c, 0][:, cols], rhs=identity[:],
                                     start=(c == 0), stop=(c == 1), is_transpose=True)

        def leave_psum(t):
            by_token[t] = made_by(scalar, [P, 4, P], F32, f"by_token{t}")
            scalar.copy(out=by_token[t][:], in_=turned[t][:])

        def turn_back(t):
            turned[t] = bank([P, 4, P], f"summed{t}")
            for b in range(4):
                nc.tensor.transpose(turned[t][:, b, :], by_token[t][:, b, :], identity[:])

        def store_turned(t):
            total = made_by(scalar, [P, T], F32, f"total{t}")
            scalar.copy(out=total[:], in_=turned[t][:].rearrange("p b i -> p (b i)"))
            scalar.dma_start(out=out[t * P:(t + 1) * P, :], in_=total[:])

        def add_and_store(t, a=0, b=T):
            total = made_by(vector, [P, b - a], F32, f"total{t}_{a}")
            vector.tensor_tensor(out=total[:], in0=parts[t, 0, a][:], in1=parts[t, 1, a][:], op=ADD)
            nc.sync.dma_start(out=out[t * P:(t + 1) * P, a:b], in_=total[:])

        regroup_w2(scalar, first, 1, first_w2[:, :, P:N])
        regroup_w2(vector, first, 0, first_w2[:, :, 0:P])
        quantise_hidden(third)
        regroup_w2(vector, second, 0, w2_raw[second, 0][:])
        quantise_w2(first, 0)
        multiply_w2(0, banks[0])
        quantise_w2(second, 0)
        regroup_w2(vector, third, 0, w2_raw[third, 0][:])
        gated(chunks(last)[0])
        regroup_w2(scalar, last, 0, w2_raw[last, 0][:])
        quantise_w2(third, 0)
        multiply_w2(0, banks[1])
        quantise_hidden(last)
        quantise_w2(last, 0)
        multiply_w2(0, banks[2])
        quantise_w2(first, 1)

        for t in range(TILES):
            following = t + 1 < TILES
            if following:
                regroup_tile(scalar, t + 1)
            bring(t)
            if 0 <= t - 2 < ADDED_BY_TENSOR:
                leave_psum(t - 2)
            if following:
                regroup_tile(vector, t + 1)
                multiply_tile(t + 1)
            if 0 <= t - 1 < ADDED_BY_TENSOR:
                turn_and_add(t - 1)
            if following:
                fetch(t, 0)
                if ADDED_BY_TENSOR <= t - 1:
                    add_and_store(t - 1)
                fetch(t, 1)
        for t in range(ADDED_BY_TENSOR):
            turn_back(t)
        for t in range(ADDED_BY_TENSOR):
            store_turned(t)

        end = TILES - 1
        fetch(end, 0, 0, CUT)
        add_and_store(end - 1)
        fetch(end, 1, 0, CUT)
        fetch(end, 0, CUT, T)
        fetch(end, 1, CUT, T)
        add_and_store(end, 0, CUT)
        add_and_store(end, CUT, T)
